import numpy as np, ml_dtypes
CORES = [1,5,17,21,33,37,49,53]
N = 8
BF = ml_dtypes.bfloat16
def gentries(a):
    return np.ascontiguousarray(a.reshape(8, 16, -1).transpose(0, 2, 1)).reshape(8, -1)
def gtable(e):
    e = np.asarray(e); return np.ascontiguousarray(e.reshape(8, -1, 16).transpose(0, 2, 1)).reshape(128, -1).astype(np.int32)
T, C, RO = 1280, 32, 2
M = 3 * T
S = (N - 1) * C
def glue(rng, w, free, slots):
    o = rng.permutation(free); n = len(slots); w[o[:n]] = M + slots; p = o[n:]
    if len(p) % 2:
        w[p[-1]] = p[-1]; p = p[:-1]
    w[p[0::2]] = p[1::2]; w[p[1::2]] = p[0::2]
def sends(w):
    at = np.zeros(S, np.int64); b = np.nonzero(w >= M)[0]; at[w[b] - M] = b
    return np.concatenate([at[(N - d - 1) * C:(N - d) * C] for d in range(1, N)])
def parts(rng):
    w = np.zeros((N, 8, M), np.int64); s = np.zeros((N, 8, S), np.int64)
    for q in range(N):
        for g in range(8):
            glue(rng, w[q, g], np.arange(M), rng.permutation(S)); s[q, g] = sends(w[q, g])
    amp = rng.choice(np.array([60.0, 150.0, 255.0]), (N, 8, 16, 1))
    X = np.rint(amp * (2 * rng.random((N, 8, 16, M)) - 1)).astype(np.int64)
    return X, w, s
def plant(rng, X, h, g):
    z = rng.integers(40, 251, (16, len(h))) * rng.choice(np.array([-1, 1]), (16, len(h)))
    for e, v in ((h, z), (g, -z)):
        X[:, e] = v; X[:, (e + T) % M] = -v; X[:, (e + 2 * T) % M] = rng.integers(-3, 4, z.shape)
def twice(rng, X, h, g):
    z = rng.choice(np.array([-1, 1]), (16, len(h))); v = rng.integers(50, 61, z.shape)
    for e, y in ((h, z), (g, -z)):
        X[:, e] = y * rng.integers(230, 251, z.shape); X[:, (e + T) % M] = rng.integers(-3, 4, z.shape); X[:, (e + 2 * T) % M] = y * v
def rivals(rng, X, w):
    n = T // 8; k = np.arange(n); o = rng.permutation(T)[:3 * n].reshape(3, n); m = k % 3; i = np.arange(16)[:, None]
    z = rng.choice(np.array([-1, 1]), (16, n)); p = rng.integers(200, 251, (16, n)); u = rng.integers(0, 101, (16, n)); used = []
    X[:, m * T + o[0]] = -z * p; X[:, ((m + 1) % 3) * T + o[0]] = -z * p; X[:, ((m + 2) % 3) * T + o[0]] = z * rng.integers(200, 256, (16, n))
    for j, few, v in ((1, (k // 3) % 5, u), (2, (k // 15) % 5, np.concatenate([u[:4], u[:3:-1]]))):
        h = ((m + j) % 3) * T + o[0]; e = rng.integers(0, 3, n) * T + o[j]; w[h] = e; w[e] = h; used += [h, e]
        y = z * (1 - 2 * (i % 2)) * rng.integers(240, 256, (16, n))
        X[:, e] = y; X[:, (e + T) % M] = -y; X[:, (e + 2 * T) % M] = z * (np.where(i < 4, (i < few).astype(np.int64), v) - p)
    glue(rng, w, np.setdiff1d(np.arange(M), np.concatenate(used)), rng.permutation(S))
def pack(X, w, s):
    return {"x": np.ascontiguousarray(X.reshape(N, 128, M)).astype(np.float32).astype(BF), "twn": w.astype(np.int32), "snd": np.stack([gtable(a) for a in s])}
def setup_inputs(rng):
    return pack(*parts(rng))
def setup_inputs_ties(rng):
    X, w, s = parts(rng)
    for g in range(8):
        if g % 4 == 0:
            X[:, g] = rng.integers(-255, 256, (1, 16, 1)); live = rng.permutation(16)[:3]
            X[:, g, live] = rng.integers(0, 2, (N, 3, M))
        elif g % 4 == 1: X[:, g] = 255 * (2 * rng.integers(0, 2, (N, 16, M)) - 1)
        elif g % 4 == 2: X[:, g] = rng.integers(-1, 2, (N, 16, M))
        else: X[:, g] = rng.integers(-255, 256, (N, 16, 1))
    for q in range(N):
        for g in (5, 6):
            rivals(rng, X[q, g], w[q, g]); s[q, g] = sends(w[q, g])
    return pack(X, w, s)
def setup_inputs_ends(rng):
    X, w, s = parts(rng)
    for q in range(N):
        glue(rng, w[q, 0], np.arange(M), np.zeros(0, np.int64))
        w[q, 1] = M + rng.integers(0, S, M)
        o = rng.permutation(M); w[q, 2, o[:T]] = o[:T]; glue(rng, w[q, 2], o[T:], rng.permutation(S))
        t = rng.permutation(T)[:T // 4]; w[q, 3, t] = T + t; w[q, 3, T + t] = t
        glue(rng, w[q, 3], np.setdiff1d(np.arange(M), np.concatenate([t, T + t])), rng.permutation(S))
        o = rng.permutation(T).reshape(2, -1)
        for i in range(3):
            a = i * T + o[0]; b = ((3 - i) % 3) * T + o[1]; w[q, 4, a] = b; w[q, 4, b] = a
        glue(rng, w[q, 5], np.arange(M), rng.choice(np.array([0, C - 1, S - 1]), T))
        w[q, 6, 0] = M - 1; w[q, 6, M - 1] = 0; glue(rng, w[q, 6], np.arange(1, M - 1), rng.permutation(S)); plant(rng, X[q, 6], np.array([0]), np.array([M - 1]))
    s[:, 0::2] = rng.choice(np.array([0, T - 1, T, 2 * T - 1, 2 * T, M - 1]), (N, 4, S)); s[:, 1::2] = rng.integers(0, M, (N, 4, S))
    return pack(X, w, s)
def setup_inputs_whirl(rng):
    X, w, s = parts(rng)
    for q in range(N):
        for g in range(8):
            o = rng.permutation(T).reshape(2, -1); p = rng.integers(0, 3, o.shape) * T + o; h, e = p[0], p[1]
            w[q, g, h] = e; w[q, g, e] = h; rest = np.setdiff1d(np.arange(M), p.reshape(-1))
            if g in (2, 6):
                b = rng.permutation((p.reshape(-1) + T) % M)[:S]
                glue(rng, w[q, g], b, rng.permutation(S)); glue(rng, w[q, g], np.setdiff1d(rest, b), np.zeros(0, np.int64))
                twice(rng, X[q, g], h, e)
            else:
                glue(rng, w[q, g], rest, rng.permutation(S))
                n = T // 2 if g % 2 == 0 else T // 4
                plant(rng, X[q, g], h[:n], e[:n])
            s[q, g] = sends(w[q, g])
        X[q, 7] = rng.integers(-255, 256, (16, 1))
    return pack(X, w, s)
def setup_inputs_mesh(rng):
    X, w, s = parts(rng); K = T // 32; cell = np.arange(16 * K).reshape(16, K)
    left = np.roll(cell, 1, axis=1).ravel(); down = np.roll(cell, -1, axis=0); right = np.roll(cell, -1, axis=1).ravel(); far = np.roll(down, -1, axis=1).ravel()
    down = down.ravel(); row = np.repeat(np.arange(16), K); col = np.tile(np.arange(K), 16); cell = cell.ravel()
    a = 2 * cell; b = a + 1; w0 = np.zeros(M, np.int64); org = np.zeros(M, np.int64)
    w0[2 * T + a] = b; w0[b] = 2 * T + a
    bl = 2 * left + 1; w0[a] = T + bl; w0[T + bl] = a
    bd = 2 * down + 1; w0[T + a] = 2 * T + bd; w0[2 * T + bd] = T + a
    org[a] = cell; org[T + a] = down; org[2 * T + a] = far; org[b] = cell; org[T + b] = far; org[2 * T + b] = right
    low = np.nonzero(w0 > np.arange(M))[0]; tri = np.arange(M) % T; side = np.arange(M) // T
    for q in range(N):
        for g in range(8):
            place = rng.permutation(T); turn = rng.integers(0, 3, T); ren = ((side + turn[tri]) % 3) * T + place[tri]
            w[q, g, ren] = ren[w0]; c = rng.permutation(low)[:S // 2]; c = np.concatenate([c, w0[c]]); w[q, g, ren[c]] = M + rng.permutation(S)
            v = 120 * np.sin(rng.random((16, 1)) * row + rng.random((16, 1)) * col + 6 * rng.random((16, 1))) + 40 * rng.standard_normal((16, 16 * K))
            X[q, g][:, ren] = np.clip(np.rint(v), -255, 255).astype(np.int64)[:, org]; s[q, g] = sends(w[q, g])
    return pack(X, w, s)
def setup_inputs_spread(rng):
    X, w, s = parts(rng)
    X = np.exp2(8 * rng.random((N, 8, 1, M))) * (rng.random((N, 8, 1, M)) > 0.0625) * (2 * rng.random((N, 8, 16, M)) - 1)
    X = np.clip(np.rint(X), -255, 255).astype(np.int64)
    for q in range(N):
        for g in range(8):
            glue(rng, w[q, g], np.arange(M), (S * rng.random(int(rng.integers(0, T))) ** 2).astype(np.int64))
    return pack(X, w, (M * rng.random((N, 8, S)) ** 3).astype(np.int64))
def check_inputs(d):
    bad = []; v = np.asarray(d["x"]).astype(np.float32); w = np.asarray(d["twn"]).astype(np.int64)
    if not (np.all(v == np.rint(v)) and np.all(np.abs(v) <= 255)): bad.append("whole numbers of x")
    for k, hi in (("twn", M + S - 1), ("snd", M - 1)):
        if np.min(d[k]) < 0 or np.max(d[k]) > hi: bad.append("range of " + k)
    back = np.take_along_axis(w, np.clip(w, 0, M - 1), 2)
    if np.any((w < M) & (back != np.arange(M))): bad.append("twins of twins in twn")
    return bad
def reference(x, twn, snd):
    X = x.astype(np.float32).astype(np.int32).reshape(N, 8, 16, M); tw = twn.astype(np.int64)
    sl = np.stack([gentries(a) for a in snd]).astype(np.int64)
    h = np.arange(M); nx = (h + T) % M; pv = (h + 2 * T) % M
    for rnd in range(RO):
        give = np.take_along_axis(X, pv[sl][:, :, None, :], 3)
        come = np.stack([np.concatenate([give[(a - d) % N][..., (d - 1) * C:d * C] for d in range(1, N)], axis=2) for a in range(N)])
        own = tw < M; t = np.minimum(tw, M - 1)
        D = np.take_along_axis(np.concatenate([X, come], axis=3), np.where(own, pv[t], tw)[:, :, None, :], 3)
        far = X[..., pv]
        gain = np.sum((X - X[..., nx]) ** 2 - (far - D) ** 2, axis=2)
        gain = np.where(own & (t % T != h % T), gain, 0).reshape(N, 8, 3, T)
        best = np.argmax(gain, axis=2)
        took = ((np.arange(3)[:, None] == best[:, :, None, :]) & (gain > 0)).reshape(N, 8, M)
        flip = took & own & np.take_along_axis(took, t, 2)
        Y = np.where(own[:, :, None, :], far, np.minimum(far, D))[..., nx]
        fn = flip[..., pv]; fp = flip[..., nx]
        loc = np.where(fn, pv[t][..., pv], np.where(fp, pv, h)); src = np.where(fn, nx, np.where(fp, nx[t][..., nx], h))
        X = np.take_along_axis(Y, np.where(flip, pv[t], src)[:, :, None, :], 3)
        e = np.take_along_axis(tw, src, 2)
        tw = np.where(e < M, np.take_along_axis(loc, np.minimum(e, M - 1), 2), e)
        sl = np.take_along_axis(loc, sl, 2)
    return {"yx": X.reshape(N, 128, M).astype(np.float32).astype(BF), "yt": tw.astype(np.float32)}

@@ -1,0 +1,493 @@
+from concourse.bass import DstId, RemoteDMATransfer
+from concourse.mybir import AluOpType, ActivationFunctionType
+
+F32, BF, I32, U16, F16 = "float32", "bfloat16", "int32", "uint16", "float16"
+NT, M, SL = 1280, 3840, 32
+SCRATCH = {
+    "ps": ("psum", [128, 4096], F32),
+    "buf0": ("sbuf", [128, 3856], BF), "buf1": ("sbuf", [128, 3856], BF), "buf2": ("sbuf", [128, 3840], BF),
+    "cb": ("sbuf", [128, 3840], BF), "sg": ("sbuf", [128, 3840], BF), "yb": ("sbuf", [128, 3840], BF),
+    "qd": ("sbuf", [128, 3840], F32), "qsq": ("sbuf", [128, 3840], F32), "lsq": ("sbuf", [128, 3840], F32),
+    "wint": ("sbuf", [128, 4096], BF), "winl": ("sbuf", [128, 4096], F32),
+    "gt": ("sbuf", [128, 1280], BF), "g16": ("sbuf", [128, 4064], F16), "g32": ("sbuf", [128, 3840], F32),
+    "slots0": ("sbuf", [128, 240], BF), "slots1": ("sbuf", [128, 240], BF),
+    "give0": ("sbuf", [128, 224], BF), "give1": ("sbuf", [128, 224], BF),
+    "twr": ("sbuf", [128, 8, 4, 16], I32), "twf": ("sbuf", [128, 4, 128], F32), "sndr": ("sbuf", [128, 16], I32),
+    "offd": ("sbuf", [128, 240], U16), "offy": ("sbuf", [128, 240], U16), "offs": ("sbuf", [128, 16], U16),
+    "offt": ("sbuf", [128, 80], U16), "offz": ("sbuf", [128, 240], U16), "offe": ("sbuf", [128, 256], U16),
+    "ha": ("sbuf", [128, 2, 352], BF), "xf": ("sbuf", [128, 240], BF),
+    "ab1": ("sbuf", [128, 240], F32), "ab2": ("sbuf", [128, 240], F32), "same": ("sbuf", [128, 240], BF),
+    "kt": ("sbuf", [128, 384], F32), "mx": ("sbuf", [128, 240], F32), "took": ("sbuf", [128, 256], BF),
+    "m1": ("sbuf", [128, 240], F32), "m2": ("sbuf", [128, 240], F32), "mp": ("sbuf", [128, 240], F32),
+    "zl": ("sbuf", [128, 480], F32), "dz": ("sbuf", [128, 240], F32), "zz": ("sbuf", [128, 240], F32),
+    "dl": ("sbuf", [128, 240], F32), "locw": ("sbuf", [128, 256], F32), "fl": ("sbuf", [128, 240], BF),
+    "n3": ("sbuf", [128, 240], F32), "n4a": ("sbuf", [128, 240], F32), "n4b": ("sbuf", [128, 240], F32),
+    "zero": ("sbuf", [128, 384], BF), "i32": ("sbuf", [128, 128], F32), "mats": ("sbuf", [128, 9, 128], BF),
+    "bsel": ("sbuf", [128, 16], F32), "ze": ("sbuf", [128, 144], BF), "ze16": ("sbuf", [128, 144], F16),
+    "zn": ("sbuf", [128, 144], BF), "pint": ("sbuf", [128, 8], I32), "pcol": ("sbuf", [128, 4], F32),
+    "k0": ("sbuf", [128, 256], F32), "ka": ("sbuf", [128, 256], F32), "kb2": ("sbuf", [128, 80], F32),
+    "sidec": ("sbuf", [128, 240], BF), "c75": ("sbuf", [128, 96], BF),
+}
+NDMA = 56
+SEMAPHORES = ["cv", "ca", "ct", "cg", "arr0", "arr1", "sent0", "sent1"] + ["d%d" % i for i in range(NDMA)]
+
+PK, PV, PE_ = 0, 338, 640
+PT = 1024
+PW, PF, PN, PP = 1536, 1776, 1856, 1936
+PA, PB = 2048, 2288
+PPI, PD1 = 2560, 2800
+PL = (3072, 3584)
+PZ, PC = 3072, 3312
+PM = 3584
+ROUND = 201326592.0
+SCALES = [1.0, -1.0, 1.0 / 4096, -1.0 / 4096, -33554432.0, 1280.0, -2560.0, 2560.0, -1280.0]
+CFG = {
+    "tch": [(0, 128), (128, 240)],
+    "qch": [(0, 40), (40, 80), (80, 128), (128, 184), (184, 216), (216, 240)],
+    "lch": [(0, 512), (512, 1024), (1024, 1280)],
+    "ych": [[(40 * j, 40 * j + 40) for j in range(6)]] * 2, "yact": [[], []],
+    "tri": [[("a", 0, 40), ("v", 40, 80)], [("a", 0, 40), ("v", 40, 80)]],
+    "x1": [("a", 0, 80), ("a", 80, 160), ("v", 160, 184), ("a", 184, 240)],
+    "x2": [("a", 0, 40), ("v", 40, 80), ("a", 80, 120), ("v", 120, 160), ("a", 160, 200), ("a", 200, 240)],
+    "tw2": [("v", 0, 130), ("a", 130, 240)],
+    "cb": [("v", 0, 512), ("v", 512, 1280), ("v", 1280, 1792), ("v", 1792, 2560), ("v", 2560, 3072), ("s", 3072, 3840)],
+    "ld": [(0, 512), (512, 1280)], "samev": [1, 1],
+}
+ORDER = [
+    21, 23, 25, 3, 10, 5, 9, 42, 46, 29, 61, 62, 26, 44, 58, 31, 32, 47, 19, 28, 63, 127, 97, 67, 98, 6, 11, 15, 4, 7, 0, 1, 2, 12, 24,
+    22, 17, 68, 70, 72, 74, 27, 18, 99, 101, 30, 69, 71, 73, 37, 43, 49, 53, 36, 13, 8, 14, 75, 77, 78, 76, 84, 102, 100, 105, 64, 106,
+    20, 103, 104, 82, 66, 79, 80, 39, 40, 41, 34, 56, 38, 57, 48, 52, 55, 33, 60, 45, 35, 81, 83, 109, 107, 86, 108, 111, 110, 112, 130,
+    113, 88, 114, 89, 131, 121, 87, 90, 122, 123, 16, 139, 129, 92, 154, 137, 125, 124, 126, 143, 138, 85, 117, 118, 94, 65, 91, 119,
+    120, 115, 116, 140, 141, 142, 136, 135, 134, 133, 132, 128, 144, 146, 54, 59, 51, 148, 149, 151, 153, 150, 145, 147, 93, 170, 155,
+    156, 157, 159, 158, 160, 162, 164, 163, 165, 167, 96, 95, 161, 152, 166, 168, 171, 172, 169, 173, 179, 181, 178, 175, 176, 180, 174,
+    182, 177, 183, 187, 188, 190, 184, 189, 192, 194, 193, 185, 195, 186, 203, 191, 196, 197, 198, 205, 201, 204, 206, 202, 199, 200,
+    207, 237, 239, 267, 214, 208, 209, 210, 238, 240, 213, 211, 241, 242, 243, 245, 244, 212, 216, 217, 247, 259, 246, 249, 215, 248,
+    251, 250, 219, 220, 50, 221, 253, 271, 270, 218, 222, 225, 255, 223, 265, 257, 263, 261, 252, 254, 256, 234, 266, 260, 258, 278,
+    276, 279, 269, 226, 277, 294, 275, 274, 272, 268, 273, 264, 227, 229, 262, 228, 230, 288, 224, 293, 290, 231, 291, 280, 283, 281,
+    282, 284, 286, 285, 287, 295, 296, 297, 299, 300, 298, 236, 235, 301, 233, 232, 302, 303, 304, 305, 307, 306, 289, 308, 312, 311,
+    309, 292, 313, 317, 319, 318, 316, 314, 327, 315, 328, 323, 320, 321, 322, 310, 329, 324, 325, 332, 330, 326, 333, 334, 341, 335,
+    331, 343, 347, 349, 339, 336, 337, 345, 338, 351, 353, 344, 348, 342, 350, 340, 346, 354, 352,
+]
+
+
+def after(core, T):
+    n = len(T.cores)
+    return [T.cores[(T.rank_of(core) + d) % n] for d in range(1, n)]
+
+
+def engine_masks(core, dsts, topo):
+    order = sorted(dsts, key=lambda c: len(topo.engines(core, c)))
+    narrow = set(topo.engines(core, order[0]))
+    used, got = set(), {c: [] for c in dsts}
+    for _ in range(2):
+        for c in order:
+            allowed = topo.engines(core, c)
+            free = [e for e in allowed if e not in used]
+            free.sort(key=lambda e: (len(allowed) > len(narrow) and e in narrow, e))
+            if free:
+                used.add(free[0])
+                got[c].append(free[0])
+    return {c: (sum(1 << e for e in es), len(es)) for c, es in got.items()}
+
+
+def transfers(core, T, topo, r):
+    dsts = after(core, T)
+    masks = engine_masks(core, dsts, topo)
+    out = []
+    for d, c in enumerate(dsts, 1):
+        rid, pid, _ = topo.addr(c)
+        out.append(RemoteDMATransfer(dst_ids=[DstId(rid=rid, pnc=pid)], dma_engine_mask=masks[c][0],
+                                     remote_sem=T.sem["arr%d" % r],
+                                     src=T["give%d" % r][:, SL * (d - 1):SL * d],
+                                     dst=T["slots%d" % r][:, 16 + SL * (d - 1):16 + SL * d]))
+    return out, sum(masks[c][1] for c in dsts)
+
+
+def rank_program(g, core, T, topo):
+    if T.rank_of(core) is None:
+        return
+    nodes = calls(g, core, T, topo)
+    assert sorted(ORDER) == list(range(len(nodes)))
+    queue = {"v": g.vector, "a": g.scalar, "t": g.tensor, "g": g, "s": g.sync}
+    count, waited, tok, ndma = {}, {q: {} for q in queue}, {}, 0
+
+    def need(q, s, n):
+        if waited[q].get(s, 0) < n:
+            queue[q].wait_ge(T.sem[s], n)
+            waited[q][s] = n
+
+    for j in ORDER:
+        nd = nodes[j]
+        q = nd["q"]
+        if nd["kind"] == "far":
+            tok[j] = nd["tok"]
+            count[tok[j][0]] = tok[j][1]
+            continue
+        best = {}
+        for d in nd["deps"]:
+            s, n = tok[d]
+            if d not in nd["soft"]:
+                best[s] = max(best.get(s, 0), n)
+        for s in sorted(best):
+            need(q, s, best[s])
+        if nd["kind"] == "send":
+            nd["fns"][0]()
+            tok[j] = nd["tok"]
+            count[tok[j][0]] = tok[j][1]
+        elif nd["kind"] == "dma":
+            tok[j] = ("d%d" % ndma, 16)
+            ndma += 1
+            nd["fns"][0]().then_inc(T.sem[tok[j][0]], 16)
+            count[tok[j][0]] = 16
+        else:
+            s = "c" + q
+            for fn in nd["fns"]:
+                fn().then_inc(T.sem[s], 1)
+                count[s] = count.get(s, 0) + 1
+            tok[j] = (s, count[s])
+    for s in sorted(count):
+        need("g", s, count[s])
+
+
+def calls(g, core, T, topo):
+    A, ACT = AluOpType, ActivationFunctionType
+    queue = {"a": g.scalar, "g": g, "s": g.sync}
+    nodes, acc, bank = [], {}, {}
+    ps = T.ps
+    TCH, QCH, LCH = CFG["tch"], CFG["qch"], CFG["lch"]
+    KW = 128 * len(TCH)
+
+    def op(q, fns, cost, reads=(), writes=(), kind="c", tok=None, deps=(), free=False):
+        j, deps = len(nodes), set(deps)
+        touched = set()
+        for xs, w in ((reads, False), (writes, True)):
+            for x in xs:
+                name, lo, hi = (x, 0, 1 << 30) if isinstance(x, str) else x
+                old = acc.get(name, [])
+                deps |= {k for a, b, k, aw in old if a < hi and lo < b and (w or aw) and k != j}
+                if w:
+                    old = [e for e in old if not (lo <= e[0] and e[1] <= hi)]
+                acc[name] = old + [(lo, hi, j, w)]
+                if name == "ps":
+                    touched |= set(range(lo // 512, (hi - 1) // 512 + 1))
+        for bk in touched:
+            owner, cur, prev = bank.get(bk, (None, [], []))
+            if owner != q:
+                cur, prev = [], cur
+            deps |= set(prev)
+            if q == "t" and not free:
+                deps |= set(cur[-1:])
+            bank[bk] = (q, cur + [j], prev)
+        soft = {d for d in deps if q == "t" and nodes[d]["q"] == "t"}
+        nodes.append({"q": q, "fns": fns, "cost": cost, "deps": deps, "soft": soft, "kind": kind, "tok": tok})
+        return j
+
+    def P(lo, n):
+        return ("ps", lo, lo + n)
+
+    def R(name, lo, n):
+        return (name, lo, lo + n)
+
+    def mms(parts, reads, writes, free=False):
+        def one(p):
+            return lambda: g.tensor.matmul(p[0], p[1], p[2], p[3], p[4])
+        return op("t", [one(p) for p in parts], (0.0, 0, 0, sum(p[5] for p in parts)), reads, writes, free=free)
+
+    def vc(n, ga=0):
+        return (0.05, 0 if ga else max(64, n), ga, 0)
+
+    def ts(out, in0, s1, s2, op0, op1, n, reads, writes, ga=0):
+        if s2 is None:
+            return op("v", [lambda: g.vector.tensor_scalar(out, in0, s1, None, op0)], vc(n, ga), reads, writes)
+        return op("v", [lambda: g.vector.tensor_scalar(out, in0, s1, s2, op0, op1)], vc(n, ga), reads, writes)
+
+    def tt(out, in0, in1, o, n, reads, writes, ga=0):
+        return op("v", [lambda: g.vector.tensor_tensor(out, in0, in1, o)], vc(n, ga), reads, writes)
+
+    def cp(out, in_, n, reads, writes, ga=0):
+        return op("v", [lambda: g.vector.tensor_copy(out, in_)], vc(n, ga), reads, writes)
+
+    def act(out, in_, f, n, reads, writes, bias=0.0, scale=1.0, ga=0):
+        return op("a", [lambda: g.scalar.activation(out, in_, f, bias=bias, scale=scale)], vc(n, ga), reads, writes)
+
+    def fill(ap, c, n, writes):
+        return op("v", [lambda: g.vector.memset(ap, c)], vc(n), (), writes)
+
+    def dma(q, out, in_, rows, size, reads, writes):
+        return op(q, [lambda: queue[q].dma_start(out, in_)], (0, rows, size, 0), reads, writes, kind="dma")
+
+    def sel(out, in_, pattern, cmp, val, base, cm, n, reads, writes):
+        return op("g", [lambda: g.affine_select(out, in_, pattern, cmp, val, base, cm)], (0.17, 2 * n, 0, 0), reads, writes)
+
+    def iota(out, pattern, base, cm, n, writes):
+        return op("g", [lambda: g.iota(out, pattern, base, cm, allow_small_or_imprecise_dtypes=True)], (0.13, 2 * n, 0, 0), (), writes)
+
+    def gather(q, out, win, off, n, reads, writes):
+        if q == "a":
+            return act(out, win.indirect(off), ACT.Identity, n, reads, writes, ga=n)
+        return cp(out, win.indirect(off), n, reads, writes, ga=n)
+
+    def mat(j):
+        return T.mats[:, j, :]
+
+    def MR(*js):
+        return [("mats", j, j + 1) for j in js]
+
+    def S(name, s, n=80):
+        return T[name][:, 80 * s:80 * s + n]
+
+    def SR(name, s, n=80):
+        return R(name, 80 * s, n)
+
+    def hs(r, s, n=80):
+        return T.ha[:, r, 14 + 80 * s:14 + 80 * s + n]
+
+    def pc(lo, n):
+        return ps[:, lo:lo + n]
+
+    HA = [("ha", 0, 254), ("ha", 1000, 1254)]
+    i32 = T.i32[:, :]
+
+    for m in range(8):
+        dma("s", T.twr[0:60, m, :, :], T.twn[m, :], 60, 15360, (), [("twr", m, m + 1)])
+    dma("s", T.sndr[:, 0:14], T.snd[:, :], 128, 7168, (), ["sndr"])
+    for lo, hi in CFG["ld"]:
+        for p in range(3):
+            s = (p + 1) % 3
+            dma("s", T.buf0[:, NT * s + lo:NT * s + hi], T.x[:, NT * p + lo:NT * p + hi], 128, 256 * (hi - lo), (),
+                [("buf0", NT * s + lo, NT * s + hi)])
+    for q, a, b in CFG["cb"]:
+        p = NT * ((a // NT + 2) % 3) + a % NT
+        if q == "s":
+            dma("s", T.cb[:, a:b], T.x[:, p:p + b - a], 128, 256 * (b - a), (), [("cb", a, b)])
+        else:
+            cp(T.cb[:, a:b], T.buf0[:, a:b], (b - a) // 2, [("buf0", a, b)], [("cb", a, b)])
+    fill(T.zero[:, :], 0.0, 192, ["zero"])
+    fill(i32, 0.0, 128, ["i32"])
+    fill(T.bsel[:, 0:8], 3.0, 8, [("bsel", 0, 8)])
+    fill(T.bsel[:, 8:16], -3.0, 8, [("bsel", 8, 16)])
+    for j in range(4):
+        fill(T.wint[:, 1024 * j:1024 * j + 1024], 0.0, 512, [("wint0", j, j + 1)])
+    op("g", [lambda: g.iota(T.pint[:, 0:1], [[0, 1]], 0, 1)], (0.13, 2, 0, 0), (), [("pint", 0, 1)])
+    sel(i32, i32, [[-1, 128]], A.not_equal, 1.0, 0, 1, 128, ["i32"], ["i32"])
+    for j in range(len(SCALES)):
+        sel(mat(j), T.zero[:, 0:128], [[-1, 128]], A.not_equal, SCALES[j], 0, 1, 128, ["zero"], MR(j))
+    sel(T.bsel[:, :], T.bsel[:, :], [[0, 2], [-16, 8]], A.is_ge, 0.0, 0, 1, 16, ["bsel"], ["bsel"])
+    sel(T.bsel[:, :], T.bsel[:, :], [[0, 2], [16, 8]], A.is_ge, 0.0, 15, -1, 16, ["bsel"], ["bsel"])
+    iota(T.k0[:, :], [[16, 256]], 0, 1, 256, ["k0"])
+    pat = [[-16, 9], [-200, 16]]
+    sel(T.ze[:, :], T.zero[:, 0:144], pat, A.not_equal, 1.0, 3000, 1, 144, ["zero"], ["ze"])
+    sel(T.zn[:, :], T.zero[:, 0:144], pat, A.not_equal, 1.0 / 4096, 2999, 1, 144, ["zero"], ["zn"])
+    sel(T.zn[:, :], T.zn[:, :], pat, A.not_equal, 1.0, 2998, 1, 144, ["zn"], ["zn"])
+    sel(T.c75[:, :], T.zero[:, 0:96], [[0, 96]], A.is_gt, -7.5, 0, 0, 96, ["zero"], ["c75"])
+    for name, lo in (("buf0", M), ("buf1", M), ("slots0", 0), ("slots1", 0)):
+        iota(T[name][:, lo:lo + 16], [[0, 16]], 16384, 0, 16, [R(name, lo, 16)])
+    iota(T.took[:, 240:256], [[0, 16]], 0, 0, 16, [("took", 240, 256)])
+    iota(T.sidec[:, :], [[-1, 3], [0, 80]], 0, 0, 240, ["sidec"])
+    for j in range(8):
+        iota(T.winl[:, 512 * j:512 * j + 512], [[0, 512]], 0, 0, 512, [("winl0", j, j + 1)])
+    ts(T.pint[:, 4:5], T.pint[:, 0:1], 112, None, A.bitwise_and, None, 1, [("pint", 0, 1)], [("pint", 4, 5)])
+    ts(T.pcol[:, 0:1], T.pint[:, 4:5], 759.5, None, A.add, None, 1, [("pint", 4, 5)], ["pcol"])
+    act(T.ka[:, :], T.k0[:, :], ACT.Identity, 256, ["k0", "pcol"], ["ka"], bias=T.pcol[:, 0:1], scale=-1.0)
+    act(T.kb2[:, :], T.ka[:, 160:240], ACT.Identity, 80, ["ka"], ["kb2"], bias=3840.0)
+    act(T.locw[:, 240:256], T.ka[:, 240:256], ACT.Identity, 16, ["ka"], [("locw", 240, 256)], bias=759.5, scale=-1.0)
+    cp(T.ze16[:, :], T.ze[:, :], 72, ["ze"], ["ze16"])
+
+    def off_d(lo, hi):
+        ts(T.offd[:, lo:hi], pc(PV + 14 + lo, hi - lo), 2039.5, 3840.0, A.add, A.min, hi - lo, [P(PV + 14 + lo, hi - lo)], [("offd", lo, hi)])
+
+    def statics(first):
+        lo = 0 if first else 14
+        n = 254 - lo
+        ts(T.ha[:, 0, lo:254], pc(PV + lo, n), ROUND, -ROUND, A.add, A.add, n, [P(PV + lo, n)], [("ha", lo, 254)])
+        tt(T.ha[:, 1, lo:254], pc(PV + lo, n), T.ha[:, 0, lo:254], A.subtract, n, [P(PV + lo, n), ("ha", lo, 254)], [("ha", 1000 + lo, 1254)])
+        ts(T.xf[:, :], pc(PV + 14, 240), -760.0, 3840.0, A.is_lt, A.mult, 240, [P(PV + 14, 240)], ["xf"])
+        ts(T.offy[:, :], pc(PV + 14, 240), -1784.5, None, A.add, None, 240, [P(PV + 14, 240)], ["offy"])
+        mms([(pc(PB, 240), mat(0), hs(0, 0, 240), True, False, 240), (pc(PB, 240), mat(0), hs(1, 0, 240), False, False, 240),
+             (pc(PB, 160), i32, T.ka[:, 0:160], False, False, 640), (pc(PB + 160, 80), i32, T.kb2[:, :], False, True, 320)],
+            HA + MR(0) + ["ka", "kb2", "i32"], [P(PB, 240)])
+        for s in range(3):
+            act(S("ab1", s), pc(PB + 80 * s, 80), ACT.Abs, 80, [P(PB + 80 * s, 80)], [SR("ab1", s)], bias=float(NT * ((s + 1) % 3) - NT))
+        act(T.ab2[:, :], T.ab1[:, :], ACT.Abs, 240, ["ab1"], ["ab2"], bias=-640.0)
+        if CFG["samev"][0 if first else 1]:
+            ts(T.same[:, :], T.ab2[:, :], 640.0, None, A.is_equal, None, 240, ["ab2"], ["same"])
+        else:
+            act(T.ab1[:, :], T.ab2[:, :], ACT.Abs, 240, ["ab2"], ["ab1"], bias=-640.0)
+            act(T.same[:, :], T.ab1[:, :], ACT.Relu, 240, ["ab1"], ["same"], bias=1.0, scale=-1.0)
+        mms([(pc(PA, 240), mat(0), hs(0, 0, 240), True, False, 240), (pc(PA, 240), mat(0), hs(1, 0, 240), False, False, 240),
+             (pc(PA, 240), mat(0), T.xf[:, :], False, False, 240), (pc(PA, 240), i32, T.ka[:, 0:240], False, True, 960)],
+            HA + MR(0) + ["ka", "xf", "i32"], [P(PA, 240)])
+        parts = [(pc(PPI, 240), mat(0), hs(1, 0, 240), True, False, 240), (pc(PPI, 240), mat(2), hs(0, 0, 240), False, True, 240)]
+        for s in range(3):
+            o = pc(PD1 + 80 * s, 80)
+            parts += [(o, mat(0), hs(1, (s + 2) % 3), True, False, 80), (o, mat(2), hs(0, (s + 2) % 3), False, False, 80),
+                      (o, mat(1), hs(1, (s + 1) % 3), False, False, 80), (o, mat(3), hs(0, (s + 1) % 3), False, True, 80)]
+        mms(parts, HA + MR(0, 1, 2, 3), [P(PPI, 480)])
+        act(T.ha[:, :, 254:350], T.ha[:, :, 14:110], ACT.Identity, 192, HA, [("ha", 254, 350), ("ha", 1254, 1350)])
+        for r in range(2):
+            dma("s", T.wint[1 + r:128:16, :], T.ha[:, r, 94:350], 128, 65536, [("ha", 1000 * r, 1000 * r + 350), "wint0"], [("wint", 1 + r, 2 + r)])
+
+    nl = [0]
+
+    def l_chunk(bn, s, lo, hi):
+        pl = PL[nl[0] % 2]
+        nl[0] += 1
+        a, b, n = NT * ((s + 1) % 3) + lo, NT * ((s + 2) % 3) + lo, hi - lo
+        mms([(pc(pl, n), mat(0), T[bn][:, a:a + n], True, False, n), (pc(pl, n), mat(1), T[bn][:, b:b + n], False, True, n)],
+            [R(bn, a, n), R(bn, b, n)] + MR(0, 1), [P(pl, n)])
+        act(T.lsq[:, NT * s + lo:NT * s + hi], pc(pl, n), ACT.Square, n, [P(pl, n)], [R("lsq", NT * s + lo, n)])
+
+    def sum_block(name, j):
+        lo, hi = TCH[j]
+        rhs = T.bsel[:, 0:8] if name == "lsq" else T.bsel[:, 8:16]
+        for i0 in range(0, 16, 4):
+            mms([(ps[0:hi - lo, PT + 128 * j + i:PT + 128 * j + 128:16], T[name][:, 16 * lo + i:16 * hi:16], rhs, False,
+                  False, 4 * min(64, hi - lo)) for i in range(i0, i0 + 4)],
+                [(name, 16 * lo, 16 * hi), "bsel", P(PT + 128 * j, 128)], (), free=True)
+
+    def gains(bn, order):
+        for lo, hi in QCH:
+            a, b = 16 * lo, 16 * hi
+            tt(T.qd[:, a:b], T[bn][:, 0:M + 16].indirect(T.offd[:, lo:hi]), T.cb[:, a:b], A.subtract, 0,
+               [bn, ("cb", a, b), ("offd", lo, hi)], [("qd", a, b)], ga=b - a)
+            act(T.qsq[:, a:b], T.qd[:, a:b], ACT.Square, b - a, [("qd", a, b)], [("qsq", a, b)])
+        mms([(pc(PT, KW), mat(0), T.zero[:, 0:KW], True, False, KW)], ["zero"] + MR(0), [P(PT, KW)])
+        for name, j in order:
+            sum_block(name, j)
+        mms([(pc(PT, 8), mat(0), T.zero[:, 0:8], False, True, 64)], ["zero"], [P(PT, KW)])
+
+    def give(bn, r):
+        gn = "give%d" % r
+        gather("a", T[gn][:, :], T[bn][:, 0:M], T.offs[:, 0:14], 224, [(bn, 0, M), "offs"], [gn])
+        tr, n = transfers(core, T, topo, r)
+        j = op("g", [lambda: g.remote_dma_fused(tr, local_sem=T.sem["sent%d" % r])], (0.3, 0, 0, 0), [gn], (), kind="send",
+               tok=("sent%d" % r, n))
+        got = sum(engine_masks(c, after(c, T), topo)[core][1] for c in T.cores if c != core)
+        op("far", [], (r, 0, 0, 0), (), [("slots%d" % r, 16, 240)], kind="far", tok=("arr%d" % r, got), deps=[j])
+
+    flag, FR = pc(PF, 80), P(PF, 80)
+
+    def choose(bn, r):
+        sn = "slots%d" % r
+        w = [P(PW, 240)]
+        mms([(pc(PW, 240), mat(0), T.sidec[:, :], True, False, 240), (pc(PW, 240), mat(4), T.same[:, :], False, False, 240)],
+            ["sidec", "same"] + MR(0, 4), w)
+        act(T.kt[:, 0:KW], pc(PT, KW), ACT.Identity, KW, [P(PT, KW)], ["kt"])
+        mms([(pc(PW + lo, hi - lo), T.kt[0:hi - lo, 128 * j:128 * j + 128], T.i32[0:hi - lo, 0:hi - lo], False, j == len(TCH) - 1,
+              4 * max(64, hi - lo)) for j, (lo, hi) in enumerate(TCH)], ["kt", "i32"], w)
+        for lo, hi in CFG["ych"][r]:
+            a, b = 16 * lo, 16 * hi
+            tt(T.yb[:, a:b], T[sn][:, :].indirect(T.offy[:, lo:hi]), T[bn][:, a:b], A.min, 0, [sn, "offy", (bn, a, b)], [("yb", a, b)], ga=b - a)
+        for k, (lo, hi) in enumerate(CFG["yact"][r]):
+            a, b = 16 * lo, 16 * hi
+            gather("a", T.sg[:, a:b], T[sn][:, :], T.offy[:, lo:hi], b - a, [sn, "offy"], [("sg", a, b)])
+            pl = PL[k % 2]
+            mms([(pc(pl, b - a), mat(0), T.sg[:, a:b], True, True, b - a)], [("sg", a, b)], [P(pl, b - a)])
+            tt(T.yb[:, a:b], pc(pl, b - a), T[bn][:, a:b], A.min, b - a, [P(pl, b - a), (bn, a, b)], [("yb", a, b)])
+        parts = []
+        for s in range(3):
+            o = pc(PM + 80 * s, 80)
+            parts += [(o, mat(1), hs(1, (s + 2) % 3), True, False, 80), (o, mat(3), hs(0, (s + 2) % 3), False, True, 80)]
+        mms(parts, HA + MR(1, 3), [P(PM, 240)])
+        key = [pc(PW + 80 * s, 80) for s in range(3)]
+        ts(S("mx", 0), key[0], 0.5, None, A.max, None, 80, w, [SR("mx", 0)])
+        tt(S("mx", 1), key[1], S("mx", 0), A.max, 80, w + [SR("mx", 0)], [SR("mx", 1)])
+        tt(S("mx", 2), key[2], S("mx", 1), A.max, 80, w + [SR("mx", 1)], [SR("mx", 2)])
+        for s in range(3):
+            tt(S("took", s), key[s], S("mx", 2), A.is_equal, 80, w + [SR("mx", 2)], [SR("took", s)])
+        dma("s", T.wint[0:128:16, :], T.took[:, :], 128, 65536, ["took", "wint0"], [("wint", 0, 1)])
+        tk = T.took[:, 0:240]
+        tt(T.mp[:, :], pc(PPI, 240), tk, A.mult, 240, [P(PPI, 240), "took"], ["mp"])
+        tt(T.m1[:, :], pc(PA, 240), tk, A.mult, 240, [P(PA, 240), "took"], ["m1"])
+        tt(T.m2[:, :], pc(PB, 240), tk, A.mult, 240, [P(PB, 240), "took"], ["m2"])
+        mms([(pc(PP, 80), i32, S("mp", s), s == 0, s == 2, 320) for s in range(3)], ["mp"], [P(PP, 80)])
+        ts(T.offt[:, :], pc(PP, 80), 256.0, 2047.0, A.mult, A.add, 80, [P(PP, 80)], ["offt"])
+        parts = []
+        for s in range(3):
+            o, j = pc(PC + 80 * s, 80), 7 if s == 0 else 8
+            parts += [(o, i32, S("m1", (s + 2) % 3), True, False, 320), (o, mat(j), S("took", (s + 2) % 3), False, False, 80),
+                      (o, mat(j), S("took", (s + 1) % 3), False, True, 80)]
+        mms(parts, ["m1", "took"] + MR(7, 8), [P(PC, 240)])
+        mms([(pc(PZ, 240), i32, T.m1[:, :], True, False, 960), (pc(PZ, 160), mat(5), S("took", 1, 160), False, False, 160),
+             (pc(PZ + 160, 80), mat(6), S("took", 0), False, False, 80), (pc(PZ + 80, 160), i32, S("m2", 0, 160), False, False, 640),
+             (pc(PZ, 80), i32, S("m2", 2), False, True, 320)], ["m1", "m2", "took"] + MR(5, 6), [P(PZ, 240)])
+        act(T.zl[:, :], pc(PZ, 480), ACT.Identity, 480, [P(PZ, 480)], ["zl"])
+        lo = 0 if r == 0 else 14
+        n, we, e0 = 254 - lo, [P(PE_, 254)], PE_ + 14
+        mms([(pc(PE_ + lo, n), mat(0), T.ha[:, 1, lo:254], True, False, n), (pc(PE_ + lo, n), mat(2), T.ha[:, 0, lo:254], False, False, n)],
+            HA + MR(0, 2), we)
+        for q, a, b in CFG["tri"][r]:
+            gather(q, T.gt[:, 16 * a:16 * b], T.wint[:, :], T.offt[:, a:b], 16 * (b - a), ["wint", "offt"], [("gt", 16 * a, 16 * b)])
+        mms([(flag, T.ze[:, 15 - i:143 - i], T.gt[:, i:NT:16], i == 0, i == 15, 80) for i in range(16)], ["gt", "ze"], [FR])
+        for s in range(3):
+            tt(S("dl", s), flag, T.zl[:, 240 + 80 * s:320 + 80 * s], A.mult, 80, [FR, "zl"], [SR("dl", s)])
+        for s in range(3):
+            tt(S("dz", s), flag, S("zl", s), A.mult, 80, [FR, "zl"], [SR("dz", s)])
+        for s in range(3):
+            tt(S("fl", s), flag, S("took", s), A.mult, 80, [FR, "took"], [SR("fl", s)])
+        tt(T.locw[:, 0:240], pc(PK, 240), T.dl[:, :], A.add, 240, [P(PK, 240), "dl"], [("locw", 0, 240)])
+        dma("s", T.winl[0:128:16, :], T.locw[:, :], 128, 131072, ["locw", "winl0"], ["winl"])
+        for s, k in ((0, 80), (1, 160)):
+            tt(S("zz", s, k), pc(PK + 80 * s, k), S("dz", s, k), A.add, k, [P(PK + 80 * s, k), SR("dz", s, k)], [SR("zz", s, k)])
+            cp(S("offz", s, k), S("zz", s, k), k, [SR("zz", s, k)], [SR("offz", s, k)])
+        mms([(pc(PN, 80), T.zn[:, 15 - i:143 - i], T.gt[:, i:NT:16], i == 0, i == 15, 80) for i in range(16)], ["gt", "zn"], [P(PN, 80)])
+        tt(T.n3[:, :], pc(PD1, 240), T.fl[:, :], A.mult, 240, [P(PD1, 240), "fl"], ["n3"])
+        mms([(pc(e0 + 80, 160), i32, S("n3", 0, 160), False, False, 640), (pc(e0, 80), i32, S("n3", 2), False, False, 320)], ["n3"], we)
+        tt(T.n4b[:, :], pc(PM, 240), T.fl[:, :], A.mult, 240, [P(PM, 240), "fl"], ["n4b"])
+        for s in range(3):
+            tt(S("n4a", s), pc(PN, 80), S("fl", s), A.mult, 80, [P(PN, 80), "fl"], [SR("n4a", s)])
+        for name in ("n4b", "n4a"):
+            mms([(pc(e0, 160), i32, S(name, 1, 160), False, False, 640), (pc(e0 + 160, 80), i32, S(name, 0), False, name == "n4a", 320)],
+                [name], we)
+        ts(T.offe[:, lo:254], pc(PE_ + lo, n), 256.0, 2047.0, A.mult, A.add, n, we, ["offe"])
+
+    def x_gather(q, bn, lo, hi):
+        gather(q, T[bn][:, 16 * lo:16 * hi], T.yb[:, :], T.offz[:, lo:hi], 16 * (hi - lo), ["yb", ("offz", lo, hi)], [(bn, 16 * lo, 16 * hi)])
+
+    nb = len(TCH)
+    sums = [("lsq", 0), ("qsq", 0)] + [("lsq", j) for j in range(1, nb)] + [("qsq", j) for j in range(1, nb)]
+
+    act(pc(PK, 240), T.ka[:, 0:240], ACT.Identity, 240, ["ka"], [P(PK, 240)], bias=759.5, scale=-1.0)
+    for b in range(4):
+        ts(T.twf[0:60, b, :], T.twr[0:60, :, b, :], -2039.5, None, A.add, None, 128, ["twr"], [("twf", b, b + 1)])
+        mms([(ps[:, PV + 14 + b:PV + 174:4], T.twf[0:60, b, :], T.i32[0:60, 0:40], True, True, 256),
+             (ps[:, PV + 174 + b:PV + 254:4], T.twf[0:60, b, :], T.i32[0:60, 40:60], True, True, 256)],
+            [("twf", b, b + 1), "i32"], [P(PV + 14, 240)])
+    cp(T.offs[:, 0:14], T.sndr[:, 0:14], 14, ["sndr"], ["offs"])
+    off_d(0, 240)
+    ts(pc(PV, 14), T.sndr[:, 0:14], -2039.5, None, A.add, None, 14, ["sndr"], [P(PV, 14)])
+    give("buf0", 0)
+    statics(True)
+    for s, k in ((0, 0), (1, 0), (2, 0), (0, 1), (0, 2), (1, 1), (1, 2), (2, 1), (2, 2)):
+        l_chunk("buf0", s, *LCH[k])
+    gains("buf0", sums)
+    choose("buf0", 0)
+    for q, lo, hi in CFG["x1"]:
+        x_gather(q, "buf1", lo, hi)
+        dma("s", T.cb[:, 16 * lo:16 * hi], T.buf1[:, 16 * lo:16 * hi], 128, 4096 * (hi - lo), [("buf1", 16 * lo, 16 * hi)], [("cb", 16 * lo, 16 * hi)])
+    for lo, hi in ((0, 94), (94, 174), (174, 254)):
+        a, b = 16 * lo, 16 * hi
+        ts(T.g16[:, a:b], T.winl[:, :].indirect(T.offe[:, lo:hi]), -2032.0, None, A.add, None, 0, ["winl", "offe"], [("g16", a, b)], ga=b - a)
+        o = pc(PV + lo, hi - lo)
+        mms([(o, mat(0), T.c75[:, 0:hi - lo], True, False, hi - lo)], ["c75"] + MR(0), [P(PV + lo, hi - lo)])
+        mms([(o, T.ze16[:, 15 - i:143 - i], T.g16[:, a + i:b:16], False, i == 15, hi - lo) for i in range(16)],
+            [("g16", a, b), "ze16"], [P(PV + lo, hi - lo)])
+    off_d(0, 160)
+    ts(T.offs[:, 0:14], pc(PV, 14), 2039.5, None, A.add, None, 14, [P(PV, 14)], ["offs"])
+    off_d(160, 240)
+    give("buf1", 1)
+    statics(False)
+    for s in range(3):
+        for k in range(3):
+            l_chunk("buf1", s, *LCH[k])
+    gains("buf1", sums)
+    choose("buf1", 1)
+    for q, lo, hi in CFG["x2"]:
+        x_gather(q, "buf2", lo, hi)
+        a = NT * ((lo // 80 + 2) % 3) + 16 * (lo % 80)
+        dma("s", T.yx[:, a:a + 16 * (hi - lo)], T.buf2[:, 16 * lo:16 * hi], 128, 4096 * (hi - lo), [("buf2", 16 * lo, 16 * hi)], ())
+    for q, lo, hi in CFG["tw2"]:
+        a, b = 16 * lo, 16 * hi
+        gather(q, T.g32[:, a:b], T.winl[:, :], T.offe[:, 14 + lo:14 + hi], b - a, ["winl", "offe"], [("g32", a, b)])
+        dma("s", T.yt[:, a:b], T.g32[0:128:16, a:b], 16, 32 * (b - a), [("g32", a, b)], ())
+    return nodes

@@ -3,33 +3,21 @@ from concourse.mybir import AluOpType, ActivationFunctionType
 
 F32, BF, I32, U16, F16 = "float32", "bfloat16", "int32", "uint16", "float16"
 NT, M, SL = 1280, 3840, 32
-SCRATCH = {
-    "ps": ("psum", [128, 4096], F32),
-    "buf0": ("sbuf", [128, 3856], BF), "buf1": ("sbuf", [128, 3856], BF), "buf2": ("sbuf", [128, 3840], BF),
-    "cb": ("sbuf", [128, 3840], BF), "sg": ("sbuf", [128, 3840], BF), "yb": ("sbuf", [128, 3840], BF),
-    "qd": ("sbuf", [128, 3840], F32), "qsq": ("sbuf", [128, 3840], F32), "lsq": ("sbuf", [128, 3840], F32),
-    "wint": ("sbuf", [128, 4096], BF), "winl": ("sbuf", [128, 4096], F32),
-    "gt": ("sbuf", [128, 1280], BF), "g16": ("sbuf", [128, 4064], F16), "g32": ("sbuf", [128, 3840], F32),
-    "slots0": ("sbuf", [128, 240], BF), "slots1": ("sbuf", [128, 240], BF),
-    "give0": ("sbuf", [128, 224], BF), "give1": ("sbuf", [128, 224], BF),
-    "twr": ("sbuf", [128, 8, 4, 16], I32), "twf": ("sbuf", [128, 4, 128], F32), "sndr": ("sbuf", [128, 16], I32),
-    "offd": ("sbuf", [128, 240], U16), "offy": ("sbuf", [128, 240], U16), "offs": ("sbuf", [128, 16], U16),
-    "offt": ("sbuf", [128, 80], U16), "offz": ("sbuf", [128, 240], U16), "offe": ("sbuf", [128, 256], U16),
-    "ha": ("sbuf", [128, 2, 352], BF), "xf": ("sbuf", [128, 240], BF),
-    "ab1": ("sbuf", [128, 240], F32), "ab2": ("sbuf", [128, 240], F32), "same": ("sbuf", [128, 240], BF),
-    "kt": ("sbuf", [128, 384], F32), "mx": ("sbuf", [128, 240], F32), "took": ("sbuf", [128, 256], BF),
-    "m1": ("sbuf", [128, 240], F32), "m2": ("sbuf", [128, 240], F32), "mp": ("sbuf", [128, 240], F32),
-    "zl": ("sbuf", [128, 480], F32), "dz": ("sbuf", [128, 240], F32), "zz": ("sbuf", [128, 240], F32),
-    "dl": ("sbuf", [128, 240], F32), "locw": ("sbuf", [128, 256], F32), "fl": ("sbuf", [128, 240], BF),
-    "n3": ("sbuf", [128, 240], F32), "n4a": ("sbuf", [128, 240], F32), "n4b": ("sbuf", [128, 240], F32),
-    "zero": ("sbuf", [128, 384], BF), "i32": ("sbuf", [128, 128], F32), "mats": ("sbuf", [128, 9, 128], BF),
-    "bsel": ("sbuf", [128, 16], F32), "ze": ("sbuf", [128, 144], BF), "ze16": ("sbuf", [128, 144], F16),
-    "zn": ("sbuf", [128, 144], BF), "pint": ("sbuf", [128, 8], I32), "pcol": ("sbuf", [128, 4], F32),
-    "k0": ("sbuf", [128, 256], F32), "ka": ("sbuf", [128, 256], F32), "kb2": ("sbuf", [128, 80], F32),
-    "sidec": ("sbuf", [128, 240], BF), "c75": ("sbuf", [128, 96], BF),
+SHAPES = {
+    BF: {"buf0": [3856], "buf1": [3856], "buf2": [3840], "cb": [3840], "sg": [3840], "yb": [3840], "wint": [4096], "gt": [1280],
+         "slots0": [240], "slots1": [240], "give0": [224], "give1": [224], "ha": [2, 352], "xf": [240], "same": [240], "took": [256],
+         "fl": [240], "zero": [384], "mats": [9, 128], "ze": [144], "zn": [144], "sidec": [240], "c75": [96]},
+    F32: {"qd": [3840], "qsq": [3840], "lsq": [3840], "winl": [4096], "g32": [3840], "twf": [4, 128], "ab1": [240], "ab2": [240],
+          "kt": [384], "mx": [240], "m1": [240], "m2": [240], "mp": [240], "zl": [480], "dz": [240], "zz": [240], "dl": [240],
+          "locw": [256], "n3": [240], "n4a": [240], "n4b": [240], "i32": [128], "bsel": [16], "pcol": [4], "k0": [256], "ka": [256],
+          "kb2": [80]},
+    F16: {"g16": [4064], "ze16": [144]},
+    I32: {"twr": [8, 4, 16], "sndr": [16], "pint": [8]},
+    U16: {"offd": [240], "offy": [240], "offs": [16], "offt": [80], "offz": [240], "offe": [256]},
 }
-NDMA = 56
-SEMAPHORES = ["cv", "ca", "ct", "cg", "arr0", "arr1", "sent0", "sent1"] + ["d%d" % i for i in range(NDMA)]
+SCRATCH = {"ps": ("psum", [128, 4096], F32)}
+SCRATCH.update({n: ("sbuf", [128] + s, d) for d in SHAPES for n, s in SHAPES[d].items()})
+SEMAPHORES = ["cv", "ca", "ct", "cg", "arr0", "arr1", "sent0", "sent1"] + ["d%d" % i for i in range(56)]
 
 PK, PV, PE_ = 0, 338, 640
 PT = 1024
@@ -43,30 +31,31 @@ ROUND = 201326592.0
 SCALES = [1.0, -1.0, 1.0 / 4096, -1.0 / 4096, -33554432.0, 1280.0, -2560.0, 2560.0, -1280.0]
 CFG = {
     "tch": [(0, 128), (128, 240)],
-    "qch": [(0, 40), (40, 80), (80, 128), (128, 184), (184, 216), (216, 240)],
+    "qch": [(0, 40), (40, 80), (80, 128), (128, 176), (176, 220), (220, 240)],
     "lch": [(0, 512), (512, 1024), (1024, 1280)],
-    "ych": [[(40 * j, 40 * j + 40) for j in range(6)]] * 2, "yact": [[], []],
+    "ych": [[(0, 36), (36, 72), (72, 108), (108, 144)]] * 2, "yact": [[(144, 176), (176, 208), (208, 240)]] * 2,
     "tri": [[("a", 0, 40), ("v", 40, 80)], [("a", 0, 40), ("v", 40, 80)]],
     "x1": [("a", 0, 80), ("a", 80, 160), ("v", 160, 184), ("a", 184, 240)],
     "x2": [("a", 0, 40), ("v", 40, 80), ("a", 80, 120), ("v", 120, 160), ("a", 160, 200), ("a", 200, 240)],
     "tw2": [("v", 0, 130), ("a", 130, 240)],
-    "cb": [("v", 0, 512), ("v", 512, 1280), ("v", 1280, 1792), ("v", 1792, 2560), ("v", 2560, 3072), ("s", 3072, 3840)],
-    "ld": [(0, 512), (512, 1280)], "samev": [1, 1],
+    "cb": [("v", 0, 512), ("s", 512, 1280), ("v", 1280, 1792), ("v", 1792, 2560), ("v", 2560, 3072), ("v", 3072, 3840)],
+    "ld": [(0, 512), (512, 1280)],
 }
 ORDER = [
-    21, 23, 25, 3, 10, 5, 9, 42, 46, 29, 61, 62, 26, 44, 58, 31, 32, 47, 19, 28, 63, 127, 97, 67, 98, 6, 11, 15, 4, 7, 0, 1, 2, 12, 24,
-    22, 17, 68, 70, 72, 74, 27, 18, 99, 101, 30, 69, 71, 73, 37, 43, 49, 53, 36, 13, 8, 14, 75, 77, 78, 76, 84, 102, 100, 105, 64, 106,
-    20, 103, 104, 82, 66, 79, 80, 39, 40, 41, 34, 56, 38, 57, 48, 52, 55, 33, 60, 45, 35, 81, 83, 109, 107, 86, 108, 111, 110, 112, 130,
-    113, 88, 114, 89, 131, 121, 87, 90, 122, 123, 16, 139, 129, 92, 154, 137, 125, 124, 126, 143, 138, 85, 117, 118, 94, 65, 91, 119,
-    120, 115, 116, 140, 141, 142, 136, 135, 134, 133, 132, 128, 144, 146, 54, 59, 51, 148, 149, 151, 153, 150, 145, 147, 93, 170, 155,
-    156, 157, 159, 158, 160, 162, 164, 163, 165, 167, 96, 95, 161, 152, 166, 168, 171, 172, 169, 173, 179, 181, 178, 175, 176, 180, 174,
-    182, 177, 183, 187, 188, 190, 184, 189, 192, 194, 193, 185, 195, 186, 203, 191, 196, 197, 198, 205, 201, 204, 206, 202, 199, 200,
-    207, 237, 239, 267, 214, 208, 209, 210, 238, 240, 213, 211, 241, 242, 243, 245, 244, 212, 216, 217, 247, 259, 246, 249, 215, 248,
-    251, 250, 219, 220, 50, 221, 253, 271, 270, 218, 222, 225, 255, 223, 265, 257, 263, 261, 252, 254, 256, 234, 266, 260, 258, 278,
-    276, 279, 269, 226, 277, 294, 275, 274, 272, 268, 273, 264, 227, 229, 262, 228, 230, 288, 224, 293, 290, 231, 291, 280, 283, 281,
-    282, 284, 286, 285, 287, 295, 296, 297, 299, 300, 298, 236, 235, 301, 233, 232, 302, 303, 304, 305, 307, 306, 289, 308, 312, 311,
-    309, 292, 313, 317, 319, 318, 316, 314, 327, 315, 328, 323, 320, 321, 322, 310, 329, 324, 325, 332, 330, 326, 333, 334, 341, 335,
-    331, 343, 347, 349, 339, 336, 337, 345, 338, 351, 353, 344, 348, 342, 350, 340, 346, 354, 352,
+    10, 9, 7, 2, 1, 11, 6, 0, 4, 5, 3, 13, 12, 8, 14, 16, 21, 23, 28, 26, 42, 47, 49, 29, 32, 31, 43, 17, 24, 22, 61, 19, 62, 15, 66,
+    70, 68, 72, 30, 33, 40, 41, 97, 98, 63, 74, 25, 18, 67, 99, 101, 127, 69, 71, 73, 75, 100, 64, 102, 103, 104, 78, 76, 84, 82, 83,
+    77, 20, 79, 105, 106, 107, 108, 86, 109, 117, 115, 110, 116, 80, 52, 34, 51, 36, 37, 54, 58, 48, 50, 38, 46, 81, 35, 44, 59, 55, 57,
+    39, 45, 60, 53, 56, 111, 130, 113, 129, 131, 114, 112, 119, 120, 87, 118, 125, 121, 126, 94, 88, 122, 123, 85, 27, 128, 138, 139,
+    136, 133, 132, 134, 135, 137, 124, 89, 90, 91, 142, 143, 140, 141, 144, 96, 95, 150, 148, 146, 145, 147, 162, 149, 163, 152, 155,
+    158, 65, 153, 93, 164, 167, 166, 165, 168, 92, 154, 177, 156, 159, 170, 169, 172, 160, 171, 173, 174, 175, 178, 157, 179, 151, 176,
+    180, 185, 189, 182, 188, 186, 181, 187, 183, 184, 161, 194, 196, 190, 195, 197, 199, 198, 200, 201, 202, 192, 203, 204, 210, 215,
+    193, 205, 191, 214, 208, 212, 206, 218, 216, 249, 217, 229, 250, 277, 225, 247, 248, 219, 220, 253, 222, 251, 252, 254, 209, 213,
+    211, 207, 224, 221, 226, 255, 257, 258, 256, 223, 228, 261, 259, 278, 281, 273, 274, 260, 230, 231, 279, 263, 227, 232, 265, 233,
+    267, 269, 235, 271, 275, 234, 299, 300, 262, 266, 264, 236, 244, 268, 239, 238, 270, 272, 287, 288, 286, 280, 276, 237, 305, 302,
+    240, 282, 283, 284, 285, 293, 291, 289, 290, 292, 294, 296, 308, 301, 241, 298, 303, 295, 246, 245, 304, 297, 312, 313, 314, 306,
+    243, 309, 317, 316, 315, 318, 319, 310, 242, 322, 320, 323, 321, 324, 325, 328, 329, 307, 330, 326, 339, 335, 336, 334, 338, 331,
+    337, 342, 333, 332, 343, 340, 356, 341, 357, 311, 346, 327, 344, 347, 345, 348, 364, 360, 366, 365, 349, 352, 351, 350, 358, 353,
+    354, 355, 362, 359, 363, 367, 361, 368, 370, 371, 369,
 ]
 
 
@@ -75,32 +64,29 @@ def after(core, T):
     return [T.cores[(T.rank_of(core) + d) % n] for d in range(1, n)]
 
 
-def engine_masks(core, dsts, topo):
-    order = sorted(dsts, key=lambda c: len(topo.engines(core, c)))
-    narrow = set(topo.engines(core, order[0]))
-    used, got = set(), {c: [] for c in dsts}
-    for _ in range(2):
-        for c in order:
-            allowed = topo.engines(core, c)
-            free = [e for e in allowed if e not in used]
-            free.sort(key=lambda e: (len(allowed) > len(narrow) and e in narrow, e))
-            if free:
-                used.add(free[0])
-                got[c].append(free[0])
-    return {c: (sum(1 << e for e in es), len(es)) for c, es in got.items()}
+def engine_sets(core, dsts, topo):
+    far = [c for c in dsts if topo.chip(c) != topo.chip(core)]
+    es = topo.engines(core, far[0])
+    k = len(es) // 4
+    cuts = [es[:2 * k], es[2 * k:3 * k], es[3 * k:], es[:k], es[k:2 * k], es[2 * k:]]
+    got = {c: (j // 3, cuts[j]) for j, c in enumerate(far)}
+    for c in dsts:
+        if c not in got:
+            got[c] = (0, [e for e in topo.engines(core, c) if e not in es][:2])
+    return got
 
 
 def transfers(core, T, topo, r):
     dsts = after(core, T)
-    masks = engine_masks(core, dsts, topo)
-    out = []
+    sets = engine_sets(core, dsts, topo)
+    out = [[], []]
     for d, c in enumerate(dsts, 1):
+        assert topo.may_write(core, c)
         rid, pid, _ = topo.addr(c)
-        out.append(RemoteDMATransfer(dst_ids=[DstId(rid=rid, pnc=pid)], dma_engine_mask=masks[c][0],
-                                     remote_sem=T.sem["arr%d" % r],
-                                     src=T["give%d" % r][:, SL * (d - 1):SL * d],
-                                     dst=T["slots%d" % r][:, 16 + SL * (d - 1):16 + SL * d]))
-    return out, sum(masks[c][1] for c in dsts)
+        out[sets[c][0]].append(RemoteDMATransfer(
+            dst_ids=[DstId(rid=rid, pnc=pid)], dma_engine_mask=sum(1 << e for e in sets[c][1]), remote_sem=T.sem["arr%d" % r],
+            src=T["give%d" % r][:, SL * (d - 1):SL * d], dst=T["slots%d" % r][:, 16 + SL * (d - 1):16 + SL * d]))
+    return out, sum(len(sets[c][1]) for c in dsts)
 
 
 def rank_program(g, core, T, topo):
@@ -109,44 +95,42 @@ def rank_program(g, core, T, topo):
     nodes = calls(g, core, T, topo)
     assert sorted(ORDER) == list(range(len(nodes)))
     queue = {"v": g.vector, "a": g.scalar, "t": g.tensor, "g": g, "s": g.sync}
-    count, waited, tok, ndma = {}, {q: {} for q in queue}, {}, 0
-
-    def need(q, s, n):
-        if waited[q].get(s, 0) < n:
-            queue[q].wait_ge(T.sem[s], n)
-            waited[q][s] = n
-
-    for j in ORDER:
+    count, last, real, tok, clock, ndma = {}, {}, {}, {}, {}, 0
+    known = {q: {} for q in queue}
+    for pos, j in enumerate(ORDER):
         nd = nodes[j]
         q = nd["q"]
         if nd["kind"] == "far":
-            tok[j] = nd["tok"]
-            count[tok[j][0]] = tok[j][1]
-            continue
-        best = {}
-        for d in nd["deps"]:
-            s, n = tok[d]
-            if d not in nd["soft"]:
-                best[s] = max(best.get(s, 0), n)
-        for s in sorted(best):
-            need(q, s, best[s])
-        if nd["kind"] == "send":
-            nd["fns"][0]()
-            tok[j] = nd["tok"]
-            count[tok[j][0]] = tok[j][1]
-        elif nd["kind"] == "dma":
-            tok[j] = ("d%d" % ndma, 16)
-            ndma += 1
-            nd["fns"][0]().then_inc(T.sem[tok[j][0]], 16)
-            count[tok[j][0]] = 16
+            tok[j], clock[j] = nd["tok"], {}
         else:
-            s = "c" + q
-            for fn in nd["fns"]:
-                fn().then_inc(T.sem[s], 1)
-                count[s] = count.get(s, 0) + 1
-            tok[j] = (s, count[s])
-    for s in sorted(count):
-        need("g", s, count[s])
+            hard = sorted((d for d in nd["deps"] if d not in nd["soft"]), key=lambda d: -last[d])
+            for d in hard:
+                s, n = tok[d]
+                if known[q].get(s, 0) < n:
+                    queue[q].wait_ge(T.sem[s], n)
+                    real[s] = max(real.get(s, 0), n)
+                    known[q][s] = n
+                    for s2, n2 in clock[d].items():
+                        known[q][s2] = max(known[q].get(s2, 0), n2)
+            clock[j] = dict(known[q])
+            if nd["kind"] == "send":
+                for fn in nd["fns"]:
+                    fn()
+                tok[j] = nd["tok"]
+            elif nd["kind"] == "dma":
+                tok[j] = ("d%d" % ndma, 16)
+                ndma += 1
+                nd["fns"][0]().then_inc(T.sem[tok[j][0]], 16)
+            else:
+                s = "c" + q
+                for fn in nd["fns"]:
+                    fn().then_inc(T.sem[s], 1)
+                tok[j] = (s, count.get(s, (0, 0))[0] + len(nd["fns"]))
+        count[tok[j][0]] = (tok[j][1], pos)
+        last[j] = pos
+    for s in sorted(count, key=lambda s: count[s][1]):
+        if real.get(s, 0) < count[s][0]:
+            g.wait_ge(T.sem[s], count[s][0])
 
 
 def calls(g, core, T, topo):
@@ -249,10 +233,10 @@ def calls(g, core, T, topo):
     i32 = T.i32[:, :]
 
     for m in range(8):
-        dma("s", T.twr[0:60, m, :, :], T.twn[m, :], 60, 15360, (), [("twr", m, m + 1)])
-    dma("s", T.sndr[:, 0:14], T.snd[:, :], 128, 7168, (), ["sndr"])
+        dma("a", T.twr[0:60, m, :, :], T.twn[m, :], 60, 15360, (), [("twr", m, m + 1)])
+    dma("a", T.sndr[:, 0:14], T.snd[:, :], 128, 7168, (), ["sndr"])
     for lo, hi in CFG["ld"]:
-        for p in range(3):
+        for p in (1, 0, 2):
             s = (p + 1) % 3
             dma("s", T.buf0[:, NT * s + lo:NT * s + hi], T.x[:, NT * p + lo:NT * p + hi], 128, 256 * (hi - lo), (),
                 [("buf0", NT * s + lo, NT * s + hi)])
@@ -309,11 +293,7 @@ def calls(g, core, T, topo):
         for s in range(3):
             act(S("ab1", s), pc(PB + 80 * s, 80), ACT.Abs, 80, [P(PB + 80 * s, 80)], [SR("ab1", s)], bias=float(NT * ((s + 1) % 3) - NT))
         act(T.ab2[:, :], T.ab1[:, :], ACT.Abs, 240, ["ab1"], ["ab2"], bias=-640.0)
-        if CFG["samev"][0 if first else 1]:
-            ts(T.same[:, :], T.ab2[:, :], 640.0, None, A.is_equal, None, 240, ["ab2"], ["same"])
-        else:
-            act(T.ab1[:, :], T.ab2[:, :], ACT.Abs, 240, ["ab2"], ["ab1"], bias=-640.0)
-            act(T.same[:, :], T.ab1[:, :], ACT.Relu, 240, ["ab1"], ["same"], bias=1.0, scale=-1.0)
+        ts(T.same[:, :], T.ab2[:, :], 640.0, None, A.is_equal, None, 240, ["ab2"], ["same"])
         mms([(pc(PA, 240), mat(0), hs(0, 0, 240), True, False, 240), (pc(PA, 240), mat(0), hs(1, 0, 240), False, False, 240),
              (pc(PA, 240), mat(0), T.xf[:, :], False, False, 240), (pc(PA, 240), i32, T.ka[:, 0:240], False, True, 960)],
             HA + MR(0) + ["ka", "xf", "i32"], [P(PA, 240)])
@@ -357,12 +337,12 @@ def calls(g, core, T, topo):
         mms([(pc(PT, 8), mat(0), T.zero[:, 0:8], False, True, 64)], ["zero"], [P(PT, KW)])
 
     def give(bn, r):
-        gn = "give%d" % r
+        gn, sent = "give%d" % r, T.sem["sent%d" % r]
         gather("a", T[gn][:, :], T[bn][:, 0:M], T.offs[:, 0:14], 224, [(bn, 0, M), "offs"], [gn])
         tr, n = transfers(core, T, topo, r)
-        j = op("g", [lambda: g.remote_dma_fused(tr, local_sem=T.sem["sent%d" % r])], (0.3, 0, 0, 0), [gn], (), kind="send",
-               tok=("sent%d" % r, n))
-        got = sum(engine_masks(c, after(c, T), topo)[core][1] for c in T.cores if c != core)
+        j = op("g", [lambda: g.remote_dma_fused(tr[0], local_sem=sent), lambda: g.remote_dma_fused(tr[1], local_sem=sent)],
+               (0.3, 0, 0, 0), [gn], (), kind="send", tok=("sent%d" % r, n))
+        got = sum(len(engine_sets(c, after(c, T), topo)[core][1]) for c in T.cores if c != core)
         op("far", [], (r, 0, 0, 0), (), [("slots%d" % r, 16, 240)], kind="far", tok=("arr%d" % r, got), deps=[j])
 
     flag, FR = pc(PF, 80), P(PF, 80)
@@ -444,8 +424,7 @@ def calls(g, core, T, topo):
     def x_gather(q, bn, lo, hi):
         gather(q, T[bn][:, 16 * lo:16 * hi], T.yb[:, :], T.offz[:, lo:hi], 16 * (hi - lo), ["yb", ("offz", lo, hi)], [(bn, 16 * lo, 16 * hi)])
 
-    nb = len(TCH)
-    sums = [("lsq", 0), ("qsq", 0)] + [("lsq", j) for j in range(1, nb)] + [("qsq", j) for j in range(1, nb)]
+    sums = [("lsq", 0), ("qsq", 0), ("lsq", 1), ("qsq", 1)]
 
     act(pc(PK, 240), T.ka[:, 0:240], ACT.Identity, 240, ["ka"], [P(PK, 240)], bias=759.5, scale=-1.0)
     for b in range(4):
@@ -465,15 +444,16 @@ def calls(g, core, T, topo):
     for q, lo, hi in CFG["x1"]:
         x_gather(q, "buf1", lo, hi)
         dma("s", T.cb[:, 16 * lo:16 * hi], T.buf1[:, 16 * lo:16 * hi], 128, 4096 * (hi - lo), [("buf1", 16 * lo, 16 * hi)], [("cb", 16 * lo, 16 * hi)])
-    for lo, hi in ((0, 94), (94, 174), (174, 254)):
+    for lo, hi in ((0, 14), (14, 94), (94, 174), (174, 254)):
         a, b = 16 * lo, 16 * hi
         ts(T.g16[:, a:b], T.winl[:, :].indirect(T.offe[:, lo:hi]), -2032.0, None, A.add, None, 0, ["winl", "offe"], [("g16", a, b)], ga=b - a)
         o = pc(PV + lo, hi - lo)
         mms([(o, mat(0), T.c75[:, 0:hi - lo], True, False, hi - lo)], ["c75"] + MR(0), [P(PV + lo, hi - lo)])
-        mms([(o, T.ze16[:, 15 - i:143 - i], T.g16[:, a + i:b:16], False, i == 15, hi - lo) for i in range(16)],
+        mms([(o, T.ze16[:, 15 - i:143 - i], T.g16[:, a + i:b:16], False, i == 15, max(64, hi - lo)) for i in range(16)],
             [("g16", a, b), "ze16"], [P(PV + lo, hi - lo)])
+        if lo == 0:
+            ts(T.offs[:, 0:14], pc(PV, 14), 2039.5, None, A.add, None, 14, [P(PV, 14)], ["offs"])
     off_d(0, 160)
-    ts(T.offs[:, 0:14], pc(PV, 14), 2039.5, None, A.add, None, 14, [P(PV, 14)], ["offs"])
     off_d(160, 240)
     give("buf1", 1)
     statics(False)

from concourse.bass import DstId, RemoteDMATransfer
from concourse.mybir import AluOpType, ActivationFunctionType

F32, BF, I32, U16, F16 = "float32", "bfloat16", "int32", "uint16", "float16"
NT, M, SL = 1280, 3840, 32
SHAPES = {
    BF: {"buf0": [3856], "buf1": [3856], "buf2": [3840], "cb": [3840], "sg": [3840], "yb": [3840], "wint": [4096], "gt": [1280],
         "slots0": [240], "slots1": [240], "give0": [224], "give1": [224], "ha": [2, 352], "xf": [240], "same": [240], "took": [256],
         "fl": [240], "zero": [384], "mats": [9, 128], "ze": [144], "zn": [144], "sidec": [240], "c75": [96]},
    F32: {"qd": [3840], "qsq": [3840], "lsq": [3840], "winl": [4096], "g32": [3840], "twf": [4, 128], "ab1": [240], "ab2": [240],
          "kt": [384], "mx": [240], "m1": [240], "m2": [240], "mp": [240], "zl": [480], "dz": [240], "zz": [240], "dl": [240],
          "locw": [256], "n3": [240], "n4a": [240], "n4b": [240], "i32": [128], "bsel": [16], "pcol": [4], "k0": [256], "ka": [256],
          "kb2": [80]},
    F16: {"g16": [4064], "ze16": [144]},
    I32: {"twr": [8, 4, 16], "sndr": [16], "pint": [8]},
    U16: {"offd": [240], "offy": [240], "offs": [16], "offt": [80], "offz": [240], "offe": [256]},
}
SCRATCH = {"ps": ("psum", [128, 4096], F32)}
SCRATCH.update({n: ("sbuf", [128] + s, d) for d in SHAPES for n, s in SHAPES[d].items()})
SEMAPHORES = ["cv", "ca", "ct", "cg", "arr0", "arr1", "sent0", "sent1"] + ["d%d" % i for i in range(56)]

PK, PV, PE_ = 0, 338, 640
PT = 1024
PW, PF, PN, PP = 1536, 1776, 1856, 1936
PA, PB = 2048, 2288
PPI, PD1 = 2560, 2800
PL = (3072, 3584)
PZ, PC = 3072, 3312
PM = 3584
ROUND = 201326592.0
SCALES = [1.0, -1.0, 1.0 / 4096, -1.0 / 4096, -33554432.0, 1280.0, -2560.0, 2560.0, -1280.0]
CFG = {
    "tch": [(0, 128), (128, 240)],
    "qch": [(0, 40), (40, 80), (80, 128), (128, 176), (176, 220), (220, 240)],
    "lch": [(0, 512), (512, 1024), (1024, 1280)],
    "ych": [[(0, 36), (36, 72), (72, 108), (108, 144)]] * 2, "yact": [[(144, 176), (176, 208), (208, 240)]] * 2,
    "tri": [[("a", 0, 40), ("v", 40, 80)], [("a", 0, 40), ("v", 40, 80)]],
    "x1": [("a", 0, 80), ("a", 80, 160), ("v", 160, 184), ("a", 184, 240)],
    "x2": [("a", 0, 40), ("v", 40, 80), ("a", 80, 120), ("v", 120, 160), ("a", 160, 200), ("a", 200, 240)],
    "tw2": [("v", 0, 130), ("a", 130, 240)],
    "cb": [("v", 0, 512), ("s", 512, 1280), ("v", 1280, 1792), ("v", 1792, 2560), ("v", 2560, 3072), ("v", 3072, 3840)],
    "ld": [(0, 512), (512, 1280)],
}
ORDER = [
    10, 9, 7, 2, 1, 11, 6, 0, 4, 5, 3, 13, 12, 8, 14, 16, 21, 23, 28, 26, 42, 47, 49, 29, 32, 31, 43, 17, 24, 22, 61, 19, 62, 15, 66,
    70, 68, 72, 30, 33, 40, 41, 97, 98, 63, 74, 25, 18, 67, 99, 101, 127, 69, 71, 73, 75, 100, 64, 102, 103, 104, 78, 76, 84, 82, 83,
    77, 20, 79, 105, 106, 107, 108, 86, 109, 117, 115, 110, 116, 80, 52, 34, 51, 36, 37, 54, 58, 48, 50, 38, 46, 81, 35, 44, 59, 55, 57,
    39, 45, 60, 53, 56, 111, 130, 113, 129, 131, 114, 112, 119, 120, 87, 118, 125, 121, 126, 94, 88, 122, 123, 85, 27, 128, 138, 139,
    136, 133, 132, 134, 135, 137, 124, 89, 90, 91, 142, 143, 140, 141, 144, 96, 95, 150, 148, 146, 145, 147, 162, 149, 163, 152, 155,
    158, 65, 153, 93, 164, 167, 166, 165, 168, 92, 154, 177, 156, 159, 170, 169, 172, 160, 171, 173, 174, 175, 178, 157, 179, 151, 176,
    180, 185, 189, 182, 188, 186, 181, 187, 183, 184, 161, 194, 196, 190, 195, 197, 199, 198, 200, 201, 202, 192, 203, 204, 210, 215,
    193, 205, 191, 214, 208, 212, 206, 218, 216, 249, 217, 229, 250, 277, 225, 247, 248, 219, 220, 253, 222, 251, 252, 254, 209, 213,
    211, 207, 224, 221, 226, 255, 257, 258, 256, 223, 228, 261, 259, 278, 281, 273, 274, 260, 230, 231, 279, 263, 227, 232, 265, 233,
    267, 269, 235, 271, 275, 234, 299, 300, 262, 266, 264, 236, 244, 268, 239, 238, 270, 272, 287, 288, 286, 280, 276, 237, 305, 302,
    240, 282, 283, 284, 285, 293, 291, 289, 290, 292, 294, 296, 308, 301, 241, 298, 303, 295, 246, 245, 304, 297, 312, 313, 314, 306,
    243, 309, 317, 316, 315, 318, 319, 310, 242, 322, 320, 323, 321, 324, 325, 328, 329, 307, 330, 326, 339, 335, 336, 334, 338, 331,
    337, 342, 333, 332, 343, 340, 356, 341, 357, 311, 346, 327, 344, 347, 345, 348, 364, 360, 366, 365, 349, 352, 351, 350, 358, 353,
    354, 355, 362, 359, 363, 367, 361, 368, 370, 371, 369,
]


def after(core, T):
    n = len(T.cores)
    return [T.cores[(T.rank_of(core) + d) % n] for d in range(1, n)]


def engine_sets(core, dsts, topo):
    far = [c for c in dsts if topo.chip(c) != topo.chip(core)]
    es = topo.engines(core, far[0])
    k = len(es) // 4
    cuts = [es[:2 * k], es[2 * k:3 * k], es[3 * k:], es[:k], es[k:2 * k], es[2 * k:]]
    got = {c: (j // 3, cuts[j]) for j, c in enumerate(far)}
    for c in dsts:
        if c not in got:
            got[c] = (0, [e for e in topo.engines(core, c) if e not in es][:2])
    return got


def transfers(core, T, topo, r):
    dsts = after(core, T)
    sets = engine_sets(core, dsts, topo)
    out = [[], []]
    for d, c in enumerate(dsts, 1):
        assert topo.may_write(core, c)
        rid, pid, _ = topo.addr(c)
        out[sets[c][0]].append(RemoteDMATransfer(
            dst_ids=[DstId(rid=rid, pnc=pid)], dma_engine_mask=sum(1 << e for e in sets[c][1]), remote_sem=T.sem["arr%d" % r],
            src=T["give%d" % r][:, SL * (d - 1):SL * d], dst=T["slots%d" % r][:, 16 + SL * (d - 1):16 + SL * d]))
    return out, sum(len(sets[c][1]) for c in dsts)


def rank_program(g, core, T, topo):
    if T.rank_of(core) is None:
        return
    nodes = calls(g, core, T, topo)
    assert sorted(ORDER) == list(range(len(nodes)))
    queue = {"v": g.vector, "a": g.scalar, "t": g.tensor, "g": g, "s": g.sync}
    count, last, real, tok, clock, ndma = {}, {}, {}, {}, {}, 0
    known = {q: {} for q in queue}
    for pos, j in enumerate(ORDER):
        nd = nodes[j]
        q = nd["q"]
        if nd["kind"] == "far":
            tok[j], clock[j] = nd["tok"], {}
        else:
            hard = sorted((d for d in nd["deps"] if d not in nd["soft"]), key=lambda d: -last[d])
            for d in hard:
                s, n = tok[d]
                if known[q].get(s, 0) < n:
                    queue[q].wait_ge(T.sem[s], n)
                    real[s] = max(real.get(s, 0), n)
                    known[q][s] = n
                    for s2, n2 in clock[d].items():
                        known[q][s2] = max(known[q].get(s2, 0), n2)
            clock[j] = dict(known[q])
            if nd["kind"] == "send":
                for fn in nd["fns"]:
                    fn()
                tok[j] = nd["tok"]
            elif nd["kind"] == "dma":
                tok[j] = ("d%d" % ndma, 16)
                ndma += 1
                nd["fns"][0]().then_inc(T.sem[tok[j][0]], 16)
            else:
                s = "c" + q
                for fn in nd["fns"]:
                    fn().then_inc(T.sem[s], 1)
                tok[j] = (s, count.get(s, (0, 0))[0] + len(nd["fns"]))
        count[tok[j][0]] = (tok[j][1], pos)
        last[j] = pos
    for s in sorted(count, key=lambda s: count[s][1]):
        if real.get(s, 0) < count[s][0]:
            g.wait_ge(T.sem[s], count[s][0])


def calls(g, core, T, topo):
    A, ACT = AluOpType, ActivationFunctionType
    queue = {"a": g.scalar, "g": g, "s": g.sync}
    nodes, acc, bank = [], {}, {}
    ps = T.ps
    TCH, QCH, LCH = CFG["tch"], CFG["qch"], CFG["lch"]
    KW = 128 * len(TCH)

    def op(q, fns, cost, reads=(), writes=(), kind="c", tok=None, deps=(), free=False):
        j, deps = len(nodes), set(deps)
        touched = set()
        for xs, w in ((reads, False), (writes, True)):
            for x in xs:
                name, lo, hi = (x, 0, 1 << 30) if isinstance(x, str) else x
                old = acc.get(name, [])
                deps |= {k for a, b, k, aw in old if a < hi and lo < b and (w or aw) and k != j}
                if w:
                    old = [e for e in old if not (lo <= e[0] and e[1] <= hi)]
                acc[name] = old + [(lo, hi, j, w)]
                if name == "ps":
                    touched |= set(range(lo // 512, (hi - 1) // 512 + 1))
        for bk in touched:
            owner, cur, prev = bank.get(bk, (None, [], []))
            if owner != q:
                cur, prev = [], cur
            deps |= set(prev)
            if q == "t" and not free:
                deps |= set(cur[-1:])
            bank[bk] = (q, cur + [j], prev)
        soft = {d for d in deps if q == "t" and nodes[d]["q"] == "t"}
        nodes.append({"q": q, "fns": fns, "cost": cost, "deps": deps, "soft": soft, "kind": kind, "tok": tok})
        return j

    def P(lo, n):
        return ("ps", lo, lo + n)

    def R(name, lo, n):
        return (name, lo, lo + n)

    def mms(parts, reads, writes, free=False):
        def one(p):
            return lambda: g.tensor.matmul(p[0], p[1], p[2], p[3], p[4])
        return op("t", [one(p) for p in parts], (0.0, 0, 0, sum(p[5] for p in parts)), reads, writes, free=free)

    def vc(n, ga=0):
        return (0.05, 0 if ga else max(64, n), ga, 0)

    def ts(out, in0, s1, s2, op0, op1, n, reads, writes, ga=0):
        if s2 is None:
            return op("v", [lambda: g.vector.tensor_scalar(out, in0, s1, None, op0)], vc(n, ga), reads, writes)
        return op("v", [lambda: g.vector.tensor_scalar(out, in0, s1, s2, op0, op1)], vc(n, ga), reads, writes)

    def tt(out, in0, in1, o, n, reads, writes, ga=0):
        return op("v", [lambda: g.vector.tensor_tensor(out, in0, in1, o)], vc(n, ga), reads, writes)

    def cp(out, in_, n, reads, writes, ga=0):
        return op("v", [lambda: g.vector.tensor_copy(out, in_)], vc(n, ga), reads, writes)

    def act(out, in_, f, n, reads, writes, bias=0.0, scale=1.0, ga=0):
        return op("a", [lambda: g.scalar.activation(out, in_, f, bias=bias, scale=scale)], vc(n, ga), reads, writes)

    def fill(ap, c, n, writes):
        return op("v", [lambda: g.vector.memset(ap, c)], vc(n), (), writes)

    def dma(q, out, in_, rows, size, reads, writes):
        return op(q, [lambda: queue[q].dma_start(out, in_)], (0, rows, size, 0), reads, writes, kind="dma")

    def sel(out, in_, pattern, cmp, val, base, cm, n, reads, writes):
        return op("g", [lambda: g.affine_select(out, in_, pattern, cmp, val, base, cm)], (0.17, 2 * n, 0, 0), reads, writes)

    def iota(out, pattern, base, cm, n, writes):
        return op("g", [lambda: g.iota(out, pattern, base, cm, allow_small_or_imprecise_dtypes=True)], (0.13, 2 * n, 0, 0), (), writes)

    def gather(q, out, win, off, n, reads, writes):
        if q == "a":
            return act(out, win.indirect(off), ACT.Identity, n, reads, writes, ga=n)
        return cp(out, win.indirect(off), n, reads, writes, ga=n)

    def mat(j):
        return T.mats[:, j, :]

    def MR(*js):
        return [("mats", j, j + 1) for j in js]

    def S(name, s, n=80):
        return T[name][:, 80 * s:80 * s + n]

    def SR(name, s, n=80):
        return R(name, 80 * s, n)

    def hs(r, s, n=80):
        return T.ha[:, r, 14 + 80 * s:14 + 80 * s + n]

    def pc(lo, n):
        return ps[:, lo:lo + n]

    HA = [("ha", 0, 254), ("ha", 1000, 1254)]
    i32 = T.i32[:, :]

    for m in range(8):
        dma("a", T.twr[0:60, m, :, :], T.twn[m, :], 60, 15360, (), [("twr", m, m + 1)])
    dma("a", T.sndr[:, 0:14], T.snd[:, :], 128, 7168, (), ["sndr"])
    for lo, hi in CFG["ld"]:
        for p in (1, 0, 2):
            s = (p + 1) % 3
            dma("s", T.buf0[:, NT * s + lo:NT * s + hi], T.x[:, NT * p + lo:NT * p + hi], 128, 256 * (hi - lo), (),
                [("buf0", NT * s + lo, NT * s + hi)])
    for q, a, b in CFG["cb"]:
        p = NT * ((a // NT + 2) % 3) + a % NT
        if q == "s":
            dma("s", T.cb[:, a:b], T.x[:, p:p + b - a], 128, 256 * (b - a), (), [("cb", a, b)])
        else:
            cp(T.cb[:, a:b], T.buf0[:, a:b], (b - a) // 2, [("buf0", a, b)], [("cb", a, b)])
    fill(T.zero[:, :], 0.0, 192, ["zero"])
    fill(i32, 0.0, 128, ["i32"])
    fill(T.bsel[:, 0:8], 3.0, 8, [("bsel", 0, 8)])
    fill(T.bsel[:, 8:16], -3.0, 8, [("bsel", 8, 16)])
    for j in range(4):
        fill(T.wint[:, 1024 * j:1024 * j + 1024], 0.0, 512, [("wint0", j, j + 1)])
    op("g", [lambda: g.iota(T.pint[:, 0:1], [[0, 1]], 0, 1)], (0.13, 2, 0, 0), (), [("pint", 0, 1)])
    sel(i32, i32, [[-1, 128]], A.not_equal, 1.0, 0, 1, 128, ["i32"], ["i32"])
    for j in range(len(SCALES)):
        sel(mat(j), T.zero[:, 0:128], [[-1, 128]], A.not_equal, SCALES[j], 0, 1, 128, ["zero"], MR(j))
    sel(T.bsel[:, :], T.bsel[:, :], [[0, 2], [-16, 8]], A.is_ge, 0.0, 0, 1, 16, ["bsel"], ["bsel"])
    sel(T.bsel[:, :], T.bsel[:, :], [[0, 2], [16, 8]], A.is_ge, 0.0, 15, -1, 16, ["bsel"], ["bsel"])
    iota(T.k0[:, :], [[16, 256]], 0, 1, 256, ["k0"])
    pat = [[-16, 9], [-200, 16]]
    sel(T.ze[:, :], T.zero[:, 0:144], pat, A.not_equal, 1.0, 3000, 1, 144, ["zero"], ["ze"])
    sel(T.zn[:, :], T.zero[:, 0:144], pat, A.not_equal, 1.0 / 4096, 2999, 1, 144, ["zero"], ["zn"])
    sel(T.zn[:, :], T.zn[:, :], pat, A.not_equal, 1.0, 2998, 1, 144, ["zn"], ["zn"])
    sel(T.c75[:, :], T.zero[:, 0:96], [[0, 96]], A.is_gt, -7.5, 0, 0, 96, ["zero"], ["c75"])
    for name, lo in (("buf0", M), ("buf1", M), ("slots0", 0), ("slots1", 0)):
        iota(T[name][:, lo:lo + 16], [[0, 16]], 16384, 0, 16, [R(name, lo, 16)])
    iota(T.took[:, 240:256], [[0, 16]], 0, 0, 16, [("took", 240, 256)])
    iota(T.sidec[:, :], [[-1, 3], [0, 80]], 0, 0, 240, ["sidec"])
    for j in range(8):
        iota(T.winl[:, 512 * j:512 * j + 512], [[0, 512]], 0, 0, 512, [("winl0", j, j + 1)])
    ts(T.pint[:, 4:5], T.pint[:, 0:1], 112, None, A.bitwise_and, None, 1, [("pint", 0, 1)], [("pint", 4, 5)])
    ts(T.pcol[:, 0:1], T.pint[:, 4:5], 759.5, None, A.add, None, 1, [("pint", 4, 5)], ["pcol"])
    act(T.ka[:, :], T.k0[:, :], ACT.Identity, 256, ["k0", "pcol"], ["ka"], bias=T.pcol[:, 0:1], scale=-1.0)
    act(T.kb2[:, :], T.ka[:, 160:240], ACT.Identity, 80, ["ka"], ["kb2"], bias=3840.0)
    act(T.locw[:, 240:256], T.ka[:, 240:256], ACT.Identity, 16, ["ka"], [("locw", 240, 256)], bias=759.5, scale=-1.0)
    cp(T.ze16[:, :], T.ze[:, :], 72, ["ze"], ["ze16"])

    def off_d(lo, hi):
        ts(T.offd[:, lo:hi], pc(PV + 14 + lo, hi - lo), 2039.5, 3840.0, A.add, A.min, hi - lo, [P(PV + 14 + lo, hi - lo)], [("offd", lo, hi)])

    def statics(first):
        lo = 0 if first else 14
        n = 254 - lo
        ts(T.ha[:, 0, lo:254], pc(PV + lo, n), ROUND, -ROUND, A.add, A.add, n, [P(PV + lo, n)], [("ha", lo, 254)])
        tt(T.ha[:, 1, lo:254], pc(PV + lo, n), T.ha[:, 0, lo:254], A.subtract, n, [P(PV + lo, n), ("ha", lo, 254)], [("ha", 1000 + lo, 1254)])
        ts(T.xf[:, :], pc(PV + 14, 240), -760.0, 3840.0, A.is_lt, A.mult, 240, [P(PV + 14, 240)], ["xf"])
        ts(T.offy[:, :], pc(PV + 14, 240), -1784.5, None, A.add, None, 240, [P(PV + 14, 240)], ["offy"])
        mms([(pc(PB, 240), mat(0), hs(0, 0, 240), True, False, 240), (pc(PB, 240), mat(0), hs(1, 0, 240), False, False, 240),
             (pc(PB, 160), i32, T.ka[:, 0:160], False, False, 640), (pc(PB + 160, 80), i32, T.kb2[:, :], False, True, 320)],
            HA + MR(0) + ["ka", "kb2", "i32"], [P(PB, 240)])
        for s in range(3):
            act(S("ab1", s), pc(PB + 80 * s, 80), ACT.Abs, 80, [P(PB + 80 * s, 80)], [SR("ab1", s)], bias=float(NT * ((s + 1) % 3) - NT))
        act(T.ab2[:, :], T.ab1[:, :], ACT.Abs, 240, ["ab1"], ["ab2"], bias=-640.0)
        ts(T.same[:, :], T.ab2[:, :], 640.0, None, A.is_equal, None, 240, ["ab2"], ["same"])
        mms([(pc(PA, 240), mat(0), hs(0, 0, 240), True, False, 240), (pc(PA, 240), mat(0), hs(1, 0, 240), False, False, 240),
             (pc(PA, 240), mat(0), T.xf[:, :], False, False, 240), (pc(PA, 240), i32, T.ka[:, 0:240], False, True, 960)],
            HA + MR(0) + ["ka", "xf", "i32"], [P(PA, 240)])
        parts = [(pc(PPI, 240), mat(0), hs(1, 0, 240), True, False, 240), (pc(PPI, 240), mat(2), hs(0, 0, 240), False, True, 240)]
        for s in range(3):
            o = pc(PD1 + 80 * s, 80)
            parts += [(o, mat(0), hs(1, (s + 2) % 3), True, False, 80), (o, mat(2), hs(0, (s + 2) % 3), False, False, 80),
                      (o, mat(1), hs(1, (s + 1) % 3), False, False, 80), (o, mat(3), hs(0, (s + 1) % 3), False, True, 80)]
        mms(parts, HA + MR(0, 1, 2, 3), [P(PPI, 480)])
        act(T.ha[:, :, 254:350], T.ha[:, :, 14:110], ACT.Identity, 192, HA, [("ha", 254, 350), ("ha", 1254, 1350)])
        for r in range(2):
            dma("s", T.wint[1 + r:128:16, :], T.ha[:, r, 94:350], 128, 65536, [("ha", 1000 * r, 1000 * r + 350), "wint0"], [("wint", 1 + r, 2 + r)])

    nl = [0]

    def l_chunk(bn, s, lo, hi):
        pl = PL[nl[0] % 2]
        nl[0] += 1
        a, b, n = NT * ((s + 1) % 3) + lo, NT * ((s + 2) % 3) + lo, hi - lo
        mms([(pc(pl, n), mat(0), T[bn][:, a:a + n], True, False, n), (pc(pl, n), mat(1), T[bn][:, b:b + n], False, True, n)],
            [R(bn, a, n), R(bn, b, n)] + MR(0, 1), [P(pl, n)])
        act(T.lsq[:, NT * s + lo:NT * s + hi], pc(pl, n), ACT.Square, n, [P(pl, n)], [R("lsq", NT * s + lo, n)])

    def sum_block(name, j):
        lo, hi = TCH[j]
        rhs = T.bsel[:, 0:8] if name == "lsq" else T.bsel[:, 8:16]
        for i0 in range(0, 16, 4):
            mms([(ps[0:hi - lo, PT + 128 * j + i:PT + 128 * j + 128:16], T[name][:, 16 * lo + i:16 * hi:16], rhs, False,
                  False, 4 * min(64, hi - lo)) for i in range(i0, i0 + 4)],
                [(name, 16 * lo, 16 * hi), "bsel", P(PT + 128 * j, 128)], (), free=True)

    def gains(bn, order):
        for lo, hi in QCH:
            a, b = 16 * lo, 16 * hi
            tt(T.qd[:, a:b], T[bn][:, 0:M + 16].indirect(T.offd[:, lo:hi]), T.cb[:, a:b], A.subtract, 0,
               [bn, ("cb", a, b), ("offd", lo, hi)], [("qd", a, b)], ga=b - a)
            act(T.qsq[:, a:b], T.qd[:, a:b], ACT.Square, b - a, [("qd", a, b)], [("qsq", a, b)])
        mms([(pc(PT, KW), mat(0), T.zero[:, 0:KW], True, False, KW)], ["zero"] + MR(0), [P(PT, KW)])
        for name, j in order:
            sum_block(name, j)
        mms([(pc(PT, 8), mat(0), T.zero[:, 0:8], False, True, 64)], ["zero"], [P(PT, KW)])

    def give(bn, r):
        gn, sent = "give%d" % r, T.sem["sent%d" % r]
        gather("a", T[gn][:, :], T[bn][:, 0:M], T.offs[:, 0:14], 224, [(bn, 0, M), "offs"], [gn])
        tr, n = transfers(core, T, topo, r)
        j = op("g", [lambda: g.remote_dma_fused(tr[0], local_sem=sent), lambda: g.remote_dma_fused(tr[1], local_sem=sent)],
               (0.3, 0, 0, 0), [gn], (), kind="send", tok=("sent%d" % r, n))
        got = sum(len(engine_sets(c, after(c, T), topo)[core][1]) for c in T.cores if c != core)
        op("far", [], (r, 0, 0, 0), (), [("slots%d" % r, 16, 240)], kind="far", tok=("arr%d" % r, got), deps=[j])

    flag, FR = pc(PF, 80), P(PF, 80)

    def choose(bn, r):
        sn = "slots%d" % r
        w = [P(PW, 240)]
        mms([(pc(PW, 240), mat(0), T.sidec[:, :], True, False, 240), (pc(PW, 240), mat(4), T.same[:, :], False, False, 240)],
            ["sidec", "same"] + MR(0, 4), w)
        act(T.kt[:, 0:KW], pc(PT, KW), ACT.Identity, KW, [P(PT, KW)], ["kt"])
        mms([(pc(PW + lo, hi - lo), T.kt[0:hi - lo, 128 * j:128 * j + 128], T.i32[0:hi - lo, 0:hi - lo], False, j == len(TCH) - 1,
              4 * max(64, hi - lo)) for j, (lo, hi) in enumerate(TCH)], ["kt", "i32"], w)
        for lo, hi in CFG["ych"][r]:
            a, b = 16 * lo, 16 * hi
            tt(T.yb[:, a:b], T[sn][:, :].indirect(T.offy[:, lo:hi]), T[bn][:, a:b], A.min, 0, [sn, "offy", (bn, a, b)], [("yb", a, b)], ga=b - a)
        for k, (lo, hi) in enumerate(CFG["yact"][r]):
            a, b = 16 * lo, 16 * hi
            gather("a", T.sg[:, a:b], T[sn][:, :], T.offy[:, lo:hi], b - a, [sn, "offy"], [("sg", a, b)])
            pl = PL[k % 2]
            mms([(pc(pl, b - a), mat(0), T.sg[:, a:b], True, True, b - a)], [("sg", a, b)], [P(pl, b - a)])
            tt(T.yb[:, a:b], pc(pl, b - a), T[bn][:, a:b], A.min, b - a, [P(pl, b - a), (bn, a, b)], [("yb", a, b)])
        parts = []
        for s in range(3):
            o = pc(PM + 80 * s, 80)
            parts += [(o, mat(1), hs(1, (s + 2) % 3), True, False, 80), (o, mat(3), hs(0, (s + 2) % 3), False, True, 80)]
        mms(parts, HA + MR(1, 3), [P(PM, 240)])
        key = [pc(PW + 80 * s, 80) for s in range(3)]
        ts(S("mx", 0), key[0], 0.5, None, A.max, None, 80, w, [SR("mx", 0)])
        tt(S("mx", 1), key[1], S("mx", 0), A.max, 80, w + [SR("mx", 0)], [SR("mx", 1)])
        tt(S("mx", 2), key[2], S("mx", 1), A.max, 80, w + [SR("mx", 1)], [SR("mx", 2)])
        for s in range(3):
            tt(S("took", s), key[s], S("mx", 2), A.is_equal, 80, w + [SR("mx", 2)], [SR("took", s)])
        dma("s", T.wint[0:128:16, :], T.took[:, :], 128, 65536, ["took", "wint0"], [("wint", 0, 1)])
        tk = T.took[:, 0:240]
        tt(T.mp[:, :], pc(PPI, 240), tk, A.mult, 240, [P(PPI, 240), "took"], ["mp"])
        tt(T.m1[:, :], pc(PA, 240), tk, A.mult, 240, [P(PA, 240), "took"], ["m1"])
        tt(T.m2[:, :], pc(PB, 240), tk, A.mult, 240, [P(PB, 240), "took"], ["m2"])
        mms([(pc(PP, 80), i32, S("mp", s), s == 0, s == 2, 320) for s in range(3)], ["mp"], [P(PP, 80)])
        ts(T.offt[:, :], pc(PP, 80), 256.0, 2047.0, A.mult, A.add, 80, [P(PP, 80)], ["offt"])
        parts = []
        for s in range(3):
            o, j = pc(PC + 80 * s, 80), 7 if s == 0 else 8
            parts += [(o, i32, S("m1", (s + 2) % 3), True, False, 320), (o, mat(j), S("took", (s + 2) % 3), False, False, 80),
                      (o, mat(j), S("took", (s + 1) % 3), False, True, 80)]
        mms(parts, ["m1", "took"] + MR(7, 8), [P(PC, 240)])
        mms([(pc(PZ, 240), i32, T.m1[:, :], True, False, 960), (pc(PZ, 160), mat(5), S("took", 1, 160), False, False, 160),
             (pc(PZ + 160, 80), mat(6), S("took", 0), False, False, 80), (pc(PZ + 80, 160), i32, S("m2", 0, 160), False, False, 640),
             (pc(PZ, 80), i32, S("m2", 2), False, True, 320)], ["m1", "m2", "took"] + MR(5, 6), [P(PZ, 240)])
        act(T.zl[:, :], pc(PZ, 480), ACT.Identity, 480, [P(PZ, 480)], ["zl"])
        lo = 0 if r == 0 else 14
        n, we, e0 = 254 - lo, [P(PE_, 254)], PE_ + 14
        mms([(pc(PE_ + lo, n), mat(0), T.ha[:, 1, lo:254], True, False, n), (pc(PE_ + lo, n), mat(2), T.ha[:, 0, lo:254], False, False, n)],
            HA + MR(0, 2), we)
        for q, a, b in CFG["tri"][r]:
            gather(q, T.gt[:, 16 * a:16 * b], T.wint[:, :], T.offt[:, a:b], 16 * (b - a), ["wint", "offt"], [("gt", 16 * a, 16 * b)])
        mms([(flag, T.ze[:, 15 - i:143 - i], T.gt[:, i:NT:16], i == 0, i == 15, 80) for i in range(16)], ["gt", "ze"], [FR])
        for s in range(3):
            tt(S("dl", s), flag, T.zl[:, 240 + 80 * s:320 + 80 * s], A.mult, 80, [FR, "zl"], [SR("dl", s)])
        for s in range(3):
            tt(S("dz", s), flag, S("zl", s), A.mult, 80, [FR, "zl"], [SR("dz", s)])
        for s in range(3):
            tt(S("fl", s), flag, S("took", s), A.mult, 80, [FR, "took"], [SR("fl", s)])
        tt(T.locw[:, 0:240], pc(PK, 240), T.dl[:, :], A.add, 240, [P(PK, 240), "dl"], [("locw", 0, 240)])
        dma("s", T.winl[0:128:16, :], T.locw[:, :], 128, 131072, ["locw", "winl0"], ["winl"])
        for s, k in ((0, 80), (1, 160)):
            tt(S("zz", s, k), pc(PK + 80 * s, k), S("dz", s, k), A.add, k, [P(PK + 80 * s, k), SR("dz", s, k)], [SR("zz", s, k)])
            cp(S("offz", s, k), S("zz", s, k), k, [SR("zz", s, k)], [SR("offz", s, k)])
        mms([(pc(PN, 80), T.zn[:, 15 - i:143 - i], T.gt[:, i:NT:16], i == 0, i == 15, 80) for i in range(16)], ["gt", "zn"], [P(PN, 80)])
        tt(T.n3[:, :], pc(PD1, 240), T.fl[:, :], A.mult, 240, [P(PD1, 240), "fl"], ["n3"])
        mms([(pc(e0 + 80, 160), i32, S("n3", 0, 160), False, False, 640), (pc(e0, 80), i32, S("n3", 2), False, False, 320)], ["n3"], we)
        tt(T.n4b[:, :], pc(PM, 240), T.fl[:, :], A.mult, 240, [P(PM, 240), "fl"], ["n4b"])
        for s in range(3):
            tt(S("n4a", s), pc(PN, 80), S("fl", s), A.mult, 80, [P(PN, 80), "fl"], [SR("n4a", s)])
        for name in ("n4b", "n4a"):
            mms([(pc(e0, 160), i32, S(name, 1, 160), False, False, 640), (pc(e0 + 160, 80), i32, S(name, 0), False, name == "n4a", 320)],
                [name], we)
        ts(T.offe[:, lo:254], pc(PE_ + lo, n), 256.0, 2047.0, A.mult, A.add, n, we, ["offe"])

    def x_gather(q, bn, lo, hi):
        gather(q, T[bn][:, 16 * lo:16 * hi], T.yb[:, :], T.offz[:, lo:hi], 16 * (hi - lo), ["yb", ("offz", lo, hi)], [(bn, 16 * lo, 16 * hi)])

    sums = [("lsq", 0), ("qsq", 0), ("lsq", 1), ("qsq", 1)]

    act(pc(PK, 240), T.ka[:, 0:240], ACT.Identity, 240, ["ka"], [P(PK, 240)], bias=759.5, scale=-1.0)
    for b in range(4):
        ts(T.twf[0:60, b, :], T.twr[0:60, :, b, :], -2039.5, None, A.add, None, 128, ["twr"], [("twf", b, b + 1)])
        mms([(ps[:, PV + 14 + b:PV + 174:4], T.twf[0:60, b, :], T.i32[0:60, 0:40], True, True, 256),
             (ps[:, PV + 174 + b:PV + 254:4], T.twf[0:60, b, :], T.i32[0:60, 40:60], True, True, 256)],
            [("twf", b, b + 1), "i32"], [P(PV + 14, 240)])
    cp(T.offs[:, 0:14], T.sndr[:, 0:14], 14, ["sndr"], ["offs"])
    off_d(0, 240)
    ts(pc(PV, 14), T.sndr[:, 0:14], -2039.5, None, A.add, None, 14, ["sndr"], [P(PV, 14)])
    give("buf0", 0)
    statics(True)
    for s, k in ((0, 0), (1, 0), (2, 0), (0, 1), (0, 2), (1, 1), (1, 2), (2, 1), (2, 2)):
        l_chunk("buf0", s, *LCH[k])
    gains("buf0", sums)
    choose("buf0", 0)
    for q, lo, hi in CFG["x1"]:
        x_gather(q, "buf1", lo, hi)
        dma("s", T.cb[:, 16 * lo:16 * hi], T.buf1[:, 16 * lo:16 * hi], 128, 4096 * (hi - lo), [("buf1", 16 * lo, 16 * hi)], [("cb", 16 * lo, 16 * hi)])
    for lo, hi in ((0, 14), (14, 94), (94, 174), (174, 254)):
        a, b = 16 * lo, 16 * hi
        ts(T.g16[:, a:b], T.winl[:, :].indirect(T.offe[:, lo:hi]), -2032.0, None, A.add, None, 0, ["winl", "offe"], [("g16", a, b)], ga=b - a)
        o = pc(PV + lo, hi - lo)
        mms([(o, mat(0), T.c75[:, 0:hi - lo], True, False, hi - lo)], ["c75"] + MR(0), [P(PV + lo, hi - lo)])
        mms([(o, T.ze16[:, 15 - i:143 - i], T.g16[:, a + i:b:16], False, i == 15, max(64, hi - lo)) for i in range(16)],
            [("g16", a, b), "ze16"], [P(PV + lo, hi - lo)])
        if lo == 0:
            ts(T.offs[:, 0:14], pc(PV, 14), 2039.5, None, A.add, None, 14, [P(PV, 14)], ["offs"])
    off_d(0, 160)
    off_d(160, 240)
    give("buf1", 1)
    statics(False)
    for s in range(3):
        for k in range(3):
            l_chunk("buf1", s, *LCH[k])
    gains("buf1", sums)
    choose("buf1", 1)
    for q, lo, hi in CFG["x2"]:
        x_gather(q, "buf2", lo, hi)
        a = NT * ((lo // 80 + 2) % 3) + 16 * (lo % 80)
        dma("s", T.yx[:, a:a + 16 * (hi - lo)], T.buf2[:, 16 * lo:16 * hi], 128, 4096 * (hi - lo), [("buf2", 16 * lo, 16 * hi)], ())
    for q, lo, hi in CFG["tw2"]:
        a, b = 16 * lo, 16 * hi
        gather(q, T.g32[:, a:b], T.winl[:, :], T.offe[:, 14 + lo:14 + hi], b - a, ["winl", "offe"], [("g32", a, b)])
        dma("s", T.yt[:, a:b], T.g32[0:128:16, a:b], 16, 32 * (b - a), [("g32", a, b)], ())
    return nodes
